import numpy as np
import ml_dtypes


def mxq(x, axis, fmt="e4m3"):
    dtype, down = {"e4m3": (ml_dtypes.float8_e4m3fn, 7), "e5m2": (ml_dtypes.float8_e5m2, 14)}[fmt]
    v = np.moveaxis(np.asarray(x, np.float32).astype(ml_dtypes.bfloat16).astype(np.float64), axis, -1)
    blocks = v.reshape(v.shape[:-1] + (-1, 32))
    amax = np.abs(blocks).max(-1, keepdims=True)
    byte = np.maximum(np.where(amax > 0, np.frexp(amax)[1] - 1 + 127, 0) - down, 1)
    scale = np.exp2(byte - 127.0)
    codes = (blocks / scale).astype(np.float32).astype(dtype).astype(np.float64)
    return np.moveaxis((codes * scale).reshape(v.shape), -1, axis)


WIDE = False


def mx_kscale(k):
    if not WIDE:
        return np.ones(k)
    levels = np.array([10, -10, 5, -5, 0])
    if k % 512:
        return np.exp2(np.random.permutation(np.resize(levels, k // 32))).repeat(32)
    a = np.empty((k // 512, 16))
    for p in range(k // 512):
        a[p, :8] = np.random.permutation(np.resize(levels, 8))
        for g in range(8):
            far = levels[np.abs(levels - a[p, g]) >= 10]
            a[p, g + 8] = far[np.random.randint(len(far))]
    return np.exp2(a.ravel()).repeat(32)


def f64(x):
    return np.asarray(x).astype(np.float64)


def striped(idx):
    return np.tile(idx.reshape(-1, 16).T, (8, 1)).astype(np.uint16)


def unstriped(offs):
    return offs[:16].T.reshape(-1).astype(np.int64)


def relu(v):
    return np.maximum(v, 0.0)


K, T, S, D, V, N = 1024, 1024, 512, 4, 256, 128
P = 2 ** 7


def setup_inputs():
    n = np.random.standard_normal
    s = mx_kscale(K)[:, None]
    return {
        "xT": (n((K, T)) * s).astype(np.float32),
        "w1": (n((K, N)) / np.sqrt(K) / s).astype(np.float32),
        "gate": (np.tile(np.random.uniform(0.2, 1.0, (D, 1, V)) / np.sqrt(D), (1, P, 1))).astype(np.float32),
        "offs": striped(np.random.permutation(T)[:S]),
        "cen": striped(np.random.permutation(S)[:V]),
        "pos1": striped(np.random.permutation(S)[:V]),
        "pos2": striped(np.random.permutation(S)[:V]),
        "pos3": striped(np.random.permutation(S)[:V]),
        "pos4": striped(np.random.permutation(S)[:V]),
    }


def reference(xT, w1, gate, offs, cen, pos1, pos2, pos3, pos4):
    xq = mxq(f64(xT)[:, unstriped(offs)], 0, "e4m3")
    y = relu(mxq(f64(w1), 0, "e4m3").T @ xq)
    yc = y[:, unstriped(cen)]
    return yc + (y[:, unstriped(pos1)] - yc) * f64(gate)[0, :1] + (y[:, unstriped(pos2)] - yc) * f64(gate)[1, :1] + (y[:, unstriped(pos3)] - yc) * f64(gate)[2, :1] + (y[:, unstriped(pos4)] - yc) * f64(gate)[3, :1]

@@ -1,0 +1,162 @@
+from contextlib import ExitStack
+
+import concourse.mybir as mybir
+from concourse.masks import make_identity
+
+K, T, S, D, V, N = 1024, 1024, 512, 4, 256, 128
+FLOPS = 2 * K * N * S
+
+F32 = mybir.dt.float32
+BF16 = mybir.dt.bfloat16
+U32 = mybir.dt.uint32
+U16 = mybir.dt.uint16
+U8 = mybir.dt.uint8
+FP8X4 = mybir.dt.float8_e4m3fn_x4
+ACT = mybir.ActivationFunctionType
+ALU = mybir.AluOpType
+
+P = 128
+PASSES = K // (4 * P)
+PIECES = ((0, 256), (256, 512))
+TURNED = 3
+CHUNKS = (
+    ((0, 512, 512), (512, 1024, 256)),
+    ((0, 512, 0), (512, 1024, 128)),
+    ((0, 512, 0), (512, 1024, 128)),
+    ((0, 512, 0), (512, 768, 0), (768, 1024, 256)),
+)
+
+
+def tile_picked_grand_relu_e_kernel(tc, xT, w1, gate, offs, cen, pos1, pos2, pos3, pos4, out):
+    nc = tc.nc
+    with ExitStack() as ctx:
+        sb = ctx.enter_context(tc.tile_pool(name="sb", bufs=1))
+        ps = ctx.enter_context(tc.psum_pool(name="ps", bufs=1))
+        turn = ctx.enter_context(tc.psum_pool(name="turn", bufs=4))
+
+        x_rows = xT.rearrange("(g p u e) t -> g u p e t", p=P, u=2, e=2)
+        w_rows = w1.rearrange("(g p j) m -> g p j m", p=P, j=4)
+
+        offs_sb = sb.tile([P, S // 16], U16, name="offs_sb")
+        raw = {}
+        for q in range(4):
+            for c, (a, b, vshare) in enumerate(CHUNKS[q]):
+                raw[q, c] = sb.tile([P, 2, b - a], F32, name="raw%d_%d" % (q, c), tag="shared" if (q, c) == (3, 1) else "raw%d_%d" % (q, c), align_bytes=64)
+                nc.sync.dma_start(out=raw[q, c][:], in_=x_rows[q // 2, q % 2, :, :, a:b])
+                if q == 0 and c == 0:
+                    nc.sync.dma_start(offs_sb[:], offs)
+        w_raw = []
+        for g in range(PASSES):
+            w_raw.append(sb.tile([P, 4, N], F32, name="w_raw%d" % g))
+            nc.sync.dma_start(out=w_raw[g][:], in_=w_rows[g])
+        gate_rows = sb.tile([P, V], F32, name="gate_rows")
+        nc.sync.dma_start(out=gate_rows[:], in_=gate.rearrange("d (r i) v -> (d r) i v", i=4)[:, 0, :])
+        lists = []
+        for i, src in enumerate((cen, pos1, pos2, pos3, pos4)):
+            lists.append(sb.tile([P, V // 16], U16, name="list%d" % i))
+            nc.sync.dma_start(lists[i][:], src)
+        gate_full = {}
+        for i in range(TURNED, D + 1):
+            gate_full[i] = sb.tile([P, V], F32, name="gate_full%d" % i)
+            nc.sync.dma_start(out=gate_full[i][:], in_=gate[i - 1])
+
+        eye = sb.tile([P, P], F32, name="eye")
+        make_identity(nc, eye[:])
+
+        pairs = [sb.tile([P, T, 2], BF16, name="pairs%d" % q, align_bytes=64) for q in range(4)]
+        picked0 = sb.tile([P, S, 4], BF16, name="picked0", align_bytes=64)
+        picked1 = sb.tile([P, S, 4], BF16, name="picked1", align_bytes=64)
+        codes0 = sb.tile([P, S], U32, name="codes0", align_bytes=64)
+        scales0 = sb.tile([P, S], U8, name="scales0", align_bytes=64)
+        scales1 = [sb.tile([P, b - a], U8, name="scales1_%d" % a, align_bytes=64) for a, b in PIECES]
+
+        def cast(q):
+            for c, (a, b, vshare) in enumerate(CHUNKS[q]):
+                src = raw[q, c][:].rearrange("p e t -> p t e")
+                split = b - a - vshare
+                if split:
+                    nc.scalar.activation(pairs[q][:, a : a + split, :], src[:, :split, :], ACT.Copy)
+                if vshare:
+                    nc.vector.tensor_copy(pairs[q][:, a + split : b, :], src[:, split:, :])
+
+        def gather(q, dst, a, b):
+            window = pairs[q][:].rearrange("p t e -> p (t e)").bitcast(U32)
+            words = dst[:].rearrange("p n j -> p (n j)").bitcast(U32).rearrange("p (n u) -> p n u", u=2)
+            nc.vector.tensor_copy(words[:, :, q % 2], window.indirect(offs_sb[:, a // 16 : b // 16]))
+
+        def quantise(codes, scales, src):
+            nc.vector.quantize_mx(out=codes[:].bitcast(FP8X4), scales=scales[:], in_=src.rearrange("p n j -> p (n j)"))
+
+        cast(0)
+        gather(0, picked0, 0, S)
+        cast(1)
+        gather(1, picked0, 0, S)
+        cast(2)
+        quantise(codes0, scales0, picked0[:])
+        gather(2, picked1, 0, S)
+        cast(3)
+
+        w_codes_both = sb.tile([P, PASSES * N], U32, name="w_codes", align_bytes=64)
+        w_scales_both = sb.tile([P, PASSES * N], U8, name="w_scales", align_bytes=64)
+        w_codes = [w_codes_both[:, g * N : (g + 1) * N] for g in range(PASSES)]
+        w_scales = [w_scales_both[:, g * N : (g + 1) * N] for g in range(PASSES)]
+        w_both = sb.tile([P, PASSES, N * 4], BF16, name="w_both", tag="shared", align_bytes=64)
+        w_bf = [w_both[:, g, :].rearrange("p (c j) -> p c j", j=4) for g in range(PASSES)]
+        for g in range(PASSES):
+            nc.scalar.copy(
+                w_bf[g].rearrange("p (c i) j -> p c j i", i=4),
+                w_raw[g][:].rearrange("p j (c i) -> p c j i", i=4),
+            )
+        gather(3, picked1, 0, S)
+        quantise(w_codes_both, w_scales_both, w_both[:].rearrange("p g (c j) -> p (g c) j", j=4))
+        codes1 = [sb.tile([P, b - a], U32, name="codes1_%d" % a, tag="shared" if i == 0 else "codes1_%d" % a, align_bytes=64) for i, (a, b) in enumerate(PIECES)]
+
+        coef = sb.tile([P, 2, D], F32, name="coef")
+        total = sb.tile([P, 2], F32, name="total")
+        stay = sb.tile([P, 2], F32, name="stay")
+        bank = turn.tile([P, 2, P], F32, name="bank")
+        for h in range(2):
+            nc.tensor.transpose(bank[:, h, :], gate_rows[:, h * P : (h + 1) * P], eye[:])
+        for h in range(2):
+            nc.scalar.activation(coef[:, h, :], bank[:, h, 0:P:32], ACT.Copy, accum_out=total[:, h : h + 1])
+        nc.scalar.activation(stay[:], total[:], ACT.Copy, scale=-1.0, bias=1.0)
+
+        y = sb.tile([P, S], F32, name="y")
+        acc = [ps.tile([P, b - a], F32, name="acc%d" % a) for a, b in PIECES]
+        for i, (a, b) in enumerate(PIECES):
+            nc.tensor.matmul_mx(out=acc[i][:], lhsT=w_codes[0].bitcast(FP8X4), lhsT_scale=w_scales[0],
+                                rhs=codes0[:, a:b].bitcast(FP8X4), rhs_scale=scales0[:, a:b], start=True, stop=False)
+        for i, (a, b) in enumerate(PIECES):
+            quantise(codes1[i], scales1[i], picked1[:, a:b, :])
+            nc.tensor.matmul_mx(out=acc[i][:], lhsT=w_codes[1].bitcast(FP8X4), lhsT_scale=w_scales[1],
+                                rhs=codes1[i][:].bitcast(FP8X4), rhs_scale=scales1[i][:], start=False, stop=True)
+            nc.scalar.activation(y[:, a:b], acc[i][:], ACT.Relu)
+
+        sums = [ps.tile([P, P], F32, name="sums%d" % h) for h in range(2)]
+
+        banks = []
+        for i in range(TURNED):
+            fetched = sb.tile([P, V], F32, name="fetched%d" % i)
+            nc.vector.tensor_copy(fetched[:], y[:].indirect(lists[i][:]))
+            banks.append(turn.tile([P, 2, P], F32, name="bank"))
+            for h in range(2):
+                nc.tensor.transpose(banks[i][:, h, :], fetched[:, h * P : (h + 1) * P], eye[:])
+        for i in range(TURNED):
+            for h in range(2):
+                scaled = sb.tile([P, P], F32, name="scaled%d_%d" % (i, h))
+                factor = stay[:, h : h + 1] if i == 0 else coef[:, h, i - 1 : i]
+                nc.scalar.activation(scaled[:], banks[i][:, h, :], ACT.Copy, scale=factor)
+                nc.tensor.matmul(sums[h][:], scaled[:], eye[:], start=(i == 0), stop=(i == TURNED - 1), is_transpose=True)
+        terms = []
+        for i in range(TURNED, D + 1):
+            terms.append(sb.tile([P, V], F32, name="term%d" % i))
+            nc.vector.tensor_tensor(terms[-1][:], y[:].indirect(lists[i][:]), gate_full[i][:], ALU.mult)
+        rest = terms[0]
+        for i, term in enumerate(terms[1:]):
+            both = sb.tile([P, V], F32, name="both%d" % i)
+            nc.vector.tensor_tensor(both[:], rest[:], term[:], ALU.add)
+            rest = both
+        for h in range(2):
+            res = sb.tile([P, P], F32, name="res%d" % h)
+            nc.vector.tensor_tensor(res[:], sums[h][:], rest[:, h * P : (h + 1) * P], ALU.add)
+            nc.sync.dma_start(out=out[:, h * P : (h + 1) * P], in_=res[:])

@@ -17,13 +17,13 @@ ALU = mybir.AluOpType
 
 P = 128
 PASSES = K // (4 * P)
-PIECES = ((0, 256), (256, 512))
+PIECES = ((0, 256), (256, 384), (384, 512))
 TURNED = 3
 CHUNKS = (
-    ((0, 512, 512), (512, 1024, 256)),
-    ((0, 512, 0), (512, 1024, 128)),
-    ((0, 512, 0), (512, 1024, 128)),
-    ((0, 512, 0), (512, 768, 0), (768, 1024, 256)),
+    ((0, 512, 512), (512, 1024, 384)),
+    ((0, 512, 0), (512, 1024, 384)),
+    ((0, 512, 0), (512, 1024, 192)),
+    ((0, 512, 0), (512, 768, 128), (768, 1024, 256)),
 )
 
 
@@ -32,7 +32,7 @@ def tile_picked_grand_relu_e_kernel(tc, xT, w1, gate, offs, cen, pos1, pos2, pos
     with ExitStack() as ctx:
         sb = ctx.enter_context(tc.tile_pool(name="sb", bufs=1))
         ps = ctx.enter_context(tc.psum_pool(name="ps", bufs=1))
-        turn = ctx.enter_context(tc.psum_pool(name="turn", bufs=4))
+        turn = ctx.enter_context(tc.psum_pool(name="turn", bufs=3))
 
         x_rows = xT.rearrange("(g p u e) t -> g u p e t", p=P, u=2, e=2)
         w_rows = w1.rearrange("(g p j) m -> g p j m", p=P, j=4)
@@ -47,7 +47,7 @@ def tile_picked_grand_relu_e_kernel(tc, xT, w1, gate, offs, cen, pos1, pos2, pos
                     nc.sync.dma_start(offs_sb[:], offs)
         w_raw = []
         for g in range(PASSES):
-            w_raw.append(sb.tile([P, 4, N], F32, name="w_raw%d" % g))
+            w_raw.append(sb.tile([P, 4, N], F32, name="w_raw%d" % g, tag="w_raw%d" % g, align_bytes=64))
             nc.sync.dma_start(out=w_raw[g][:], in_=w_rows[g])
         gate_rows = sb.tile([P, V], F32, name="gate_rows")
         nc.sync.dma_start(out=gate_rows[:], in_=gate.rearrange("d (r i) v -> (d r) i v", i=4)[:, 0, :])
@@ -85,52 +85,52 @@ def tile_picked_grand_relu_e_kernel(tc, xT, w1, gate, offs, cen, pos1, pos2, pos
             nc.vector.tensor_copy(words[:, :, q % 2], window.indirect(offs_sb[:, a // 16 : b // 16]))
 
         def quantise(codes, scales, src):
-            nc.vector.quantize_mx(out=codes[:].bitcast(FP8X4), scales=scales[:], in_=src.rearrange("p n j -> p (n j)"))
+            nc.vector.quantize_mx(out=codes.bitcast(FP8X4), scales=scales[:], in_=src.rearrange("p n j -> p (n j)"))
 
         cast(0)
         gather(0, picked0, 0, S)
         cast(1)
         gather(1, picked0, 0, S)
         cast(2)
-        quantise(codes0, scales0, picked0[:])
+        quantise(codes0[:], scales0, picked0[:])
         gather(2, picked1, 0, S)
         cast(3)
 
-        w_codes_both = sb.tile([P, PASSES * N], U32, name="w_codes", align_bytes=64)
-        w_scales_both = sb.tile([P, PASSES * N], U8, name="w_scales", align_bytes=64)
-        w_codes = [w_codes_both[:, g * N : (g + 1) * N] for g in range(PASSES)]
-        w_scales = [w_scales_both[:, g * N : (g + 1) * N] for g in range(PASSES)]
+        w_codes, w_scales = [], []
         w_both = sb.tile([P, PASSES, N * 4], BF16, name="w_both", tag="shared", align_bytes=64)
         w_bf = [w_both[:, g, :].rearrange("p (c j) -> p c j", j=4) for g in range(PASSES)]
         for g in range(PASSES):
+            w_codes.append(sb.tile([P, N], U32, name="w_codes%d" % g, align_bytes=64))
+            w_scales.append(sb.tile([P, N], U8, name="w_scales%d" % g, align_bytes=64))
             nc.scalar.copy(
                 w_bf[g].rearrange("p (c i) j -> p c j i", i=4),
                 w_raw[g][:].rearrange("p j (c i) -> p c j i", i=4),
             )
         gather(3, picked1, 0, S)
-        quantise(w_codes_both, w_scales_both, w_both[:].rearrange("p g (c j) -> p (g c) j", j=4))
-        codes1 = [sb.tile([P, b - a], U32, name="codes1_%d" % a, tag="shared" if i == 0 else "codes1_%d" % a, align_bytes=64) for i, (a, b) in enumerate(PIECES)]
+        for g in range(PASSES):
+            quantise(w_codes[g][:], w_scales[g], w_bf[g])
+        codes1 = sb.tile([P, S], U32, name="codes1", tag="w_raw1", align_bytes=64)
+
+        y = sb.tile([P, S], F32, name="y")
+        acc = [ps.tile([P, b - a], F32, name="acc%d" % a, tag="acc%d" % a) for a, b in PIECES]
+        for i, (a, b) in enumerate(PIECES):
+            nc.tensor.matmul_mx(out=acc[i][:], lhsT=w_codes[0][:].bitcast(FP8X4), lhsT_scale=w_scales[0][:],
+                                rhs=codes0[:, a:b].bitcast(FP8X4), rhs_scale=scales0[:, a:b], start=True, stop=False)
+        for i, (a, b) in enumerate(PIECES):
+            quantise(codes1[:, a:b], scales1[i], picked1[:, a:b, :])
+            nc.tensor.matmul_mx(out=acc[i][:], lhsT=w_codes[1][:].bitcast(FP8X4), lhsT_scale=w_scales[1][:],
+                                rhs=codes1[:, a:b].bitcast(FP8X4), rhs_scale=scales1[i][:], start=False, stop=True)
+            nc.scalar.activation(y[:, a:b], acc[i][:], ACT.Relu)
 
         coef = sb.tile([P, 2, D], F32, name="coef")
         total = sb.tile([P, 2], F32, name="total")
         stay = sb.tile([P, 2], F32, name="stay")
-        bank = turn.tile([P, 2, P], F32, name="bank")
+        bank = ps.tile([P, 2, P], F32, name="gate_bank", tag="acc%d" % PIECES[-1][0])
         for h in range(2):
             nc.tensor.transpose(bank[:, h, :], gate_rows[:, h * P : (h + 1) * P], eye[:])
         for h in range(2):
             nc.scalar.activation(coef[:, h, :], bank[:, h, 0:P:32], ACT.Copy, accum_out=total[:, h : h + 1])
         nc.scalar.activation(stay[:], total[:], ACT.Copy, scale=-1.0, bias=1.0)
-
-        y = sb.tile([P, S], F32, name="y")
-        acc = [ps.tile([P, b - a], F32, name="acc%d" % a) for a, b in PIECES]
-        for i, (a, b) in enumerate(PIECES):
-            nc.tensor.matmul_mx(out=acc[i][:], lhsT=w_codes[0].bitcast(FP8X4), lhsT_scale=w_scales[0],
-                                rhs=codes0[:, a:b].bitcast(FP8X4), rhs_scale=scales0[:, a:b], start=True, stop=False)
-        for i, (a, b) in enumerate(PIECES):
-            quantise(codes1[i], scales1[i], picked1[:, a:b, :])
-            nc.tensor.matmul_mx(out=acc[i][:], lhsT=w_codes[1].bitcast(FP8X4), lhsT_scale=w_scales[1],
-                                rhs=codes1[i][:].bitcast(FP8X4), rhs_scale=scales1[i][:], start=False, stop=True)
-            nc.scalar.activation(y[:, a:b], acc[i][:], ACT.Relu)
 
         sums = [ps.tile([P, P], F32, name="sums%d" % h) for h in range(2)]
 

@@ -8,6 +8,7 @@ FLOPS = 2 * K * N * S
 
 F32 = mybir.dt.float32
 BF16 = mybir.dt.bfloat16
+I32 = mybir.dt.int32
 U32 = mybir.dt.uint32
 U16 = mybir.dt.uint16
 U8 = mybir.dt.uint8
@@ -22,8 +23,8 @@ TURNED = 3
 CHUNKS = (
     ((0, 512, 512), (512, 1024, 384)),
     ((0, 512, 0), (512, 1024, 384)),
-    ((0, 512, 0), (512, 1024, 192)),
-    ((0, 512, 0), (512, 768, 128), (768, 1024, 256)),
+    ((0, 512, 0), (512, 1024, 128)),
+    ((0, 512, 0), (512, 768, 0), (768, 1024, 256)),
 )
 
 
@@ -32,25 +33,25 @@ def tile_picked_grand_relu_e_kernel(tc, xT, w1, gate, offs, cen, pos1, pos2, pos
     with ExitStack() as ctx:
         sb = ctx.enter_context(tc.tile_pool(name="sb", bufs=1))
         ps = ctx.enter_context(tc.psum_pool(name="ps", bufs=1))
-        turn = ctx.enter_context(tc.psum_pool(name="turn", bufs=3))
 
         x_rows = xT.rearrange("(g p u e) t -> g u p e t", p=P, u=2, e=2)
         w_rows = w1.rearrange("(g p j) m -> g p j m", p=P, j=4)
 
         offs_sb = sb.tile([P, S // 16], U16, name="offs_sb")
+        gate_rows = sb.tile([P, V], F32, name="gate_rows")
+        nc.gpsimd.memset(gate_rows[:], 0.0)
         raw = {}
         for q in range(4):
             for c, (a, b, vshare) in enumerate(CHUNKS[q]):
-                raw[q, c] = sb.tile([P, 2, b - a], F32, name="raw%d_%d" % (q, c), tag="shared" if (q, c) == (3, 1) else "raw%d_%d" % (q, c), align_bytes=64)
+                raw[q, c] = sb.tile([P, 2, b - a], F32, name="raw%d_%d" % (q, c), tag="raw%d_%d" % (q, c), align_bytes=64)
                 nc.sync.dma_start(out=raw[q, c][:], in_=x_rows[q // 2, q % 2, :, :, a:b])
                 if q == 0 and c == 0:
                     nc.sync.dma_start(offs_sb[:], offs)
+                    nc.sync.dma_start(out=gate_rows[0:D, :], in_=gate[:, 0, :])
         w_raw = []
         for g in range(PASSES):
             w_raw.append(sb.tile([P, 4, N], F32, name="w_raw%d" % g, tag="w_raw%d" % g, align_bytes=64))
             nc.sync.dma_start(out=w_raw[g][:], in_=w_rows[g])
-        gate_rows = sb.tile([P, V], F32, name="gate_rows")
-        nc.sync.dma_start(out=gate_rows[:], in_=gate.rearrange("d (r i) v -> (d r) i v", i=4)[:, 0, :])
         lists = []
         for i, src in enumerate((cen, pos1, pos2, pos3, pos4)):
             lists.append(sb.tile([P, V // 16], U16, name="list%d" % i))
@@ -65,10 +66,11 @@ def tile_picked_grand_relu_e_kernel(tc, xT, w1, gate, offs, cen, pos1, pos2, pos
 
         pairs = [sb.tile([P, T, 2], BF16, name="pairs%d" % q, align_bytes=64) for q in range(4)]
         picked0 = sb.tile([P, S, 4], BF16, name="picked0", align_bytes=64)
-        picked1 = sb.tile([P, S, 4], BF16, name="picked1", align_bytes=64)
+        words1 = sb.tile([P, 2, S], U32, name="words1")
+        words0 = sb.tile([P, 2, S], U32, name="words0")
         codes0 = sb.tile([P, S], U32, name="codes0", align_bytes=64)
         scales0 = sb.tile([P, S], U8, name="scales0", align_bytes=64)
-        scales1 = [sb.tile([P, b - a], U8, name="scales1_%d" % a, align_bytes=64) for a, b in PIECES]
+        scales1 = sb.tile([P, S], U8, name="scales1", align_bytes=64)
 
         def cast(q):
             for c, (a, b, vshare) in enumerate(CHUNKS[q]):
@@ -79,84 +81,96 @@ def tile_picked_grand_relu_e_kernel(tc, xT, w1, gate, offs, cen, pos1, pos2, pos
                 if vshare:
                     nc.vector.tensor_copy(pairs[q][:, a + split : b, :], src[:, split:, :])
 
-        def gather(q, dst, a, b):
-            window = pairs[q][:].rearrange("p t e -> p (t e)").bitcast(U32)
+        def window(q):
+            return pairs[q][:].rearrange("p t e -> p (t e)").bitcast(U32)
+
+        def gather(q, dst):
             words = dst[:].rearrange("p n j -> p (n j)").bitcast(U32).rearrange("p (n u) -> p n u", u=2)
-            nc.vector.tensor_copy(words[:, :, q % 2], window.indirect(offs_sb[:, a // 16 : b // 16]))
+            nc.vector.tensor_copy(words[:, :, q % 2], window(q).indirect(offs_sb[:]))
+
+        def gather_plain(q, words, a, b):
+            nc.vector.tensor_copy(words[:, q % 2, a:b], window(q).indirect(offs_sb[:, a // 16 : b // 16]))
+
+        def weave(words, dst, a, b):
+            woven = dst[:, a:b, :].rearrange("p n j -> p (n j)").bitcast(I32).rearrange("p (n u) -> p n u", u=2)
+            nc.vector.tensor_copy(woven, words[:, :, a:b].bitcast(I32).rearrange("p u n -> p n u"))
 
         def quantise(codes, scales, src):
-            nc.vector.quantize_mx(out=codes.bitcast(FP8X4), scales=scales[:], in_=src.rearrange("p n j -> p (n j)"))
+            nc.vector.quantize_mx(out=codes.bitcast(FP8X4), scales=scales, in_=src.rearrange("p n j -> p (n j)"))
 
         cast(0)
-        gather(0, picked0, 0, S)
+        gather_plain(0, words0, 0, S)
         cast(1)
-        gather(1, picked0, 0, S)
+        gather_plain(1, words0, 0, S)
+        weave(words0, picked0, 0, S)
         cast(2)
-        quantise(codes0[:], scales0, picked0[:])
-        gather(2, picked1, 0, S)
+        quantise(codes0[:], scales0[:], picked0[:])
+        gather_plain(2, words1, 0, S)
         cast(3)
 
-        w_codes, w_scales = [], []
-        w_both = sb.tile([P, PASSES, N * 4], BF16, name="w_both", tag="shared", align_bytes=64)
-        w_bf = [w_both[:, g, :].rearrange("p (c j) -> p c j", j=4) for g in range(PASSES)]
+        w_bf = sb.tile([P, PASSES * N, 4], BF16, name="w_bf", tag="raw3_1", align_bytes=64)
+        w_codes = sb.tile([P, PASSES * N], U32, name="w_codes", align_bytes=64)
+        w_scales = sb.tile([P, PASSES * N], U8, name="w_scales", align_bytes=64)
         for g in range(PASSES):
-            w_codes.append(sb.tile([P, N], U32, name="w_codes%d" % g, align_bytes=64))
-            w_scales.append(sb.tile([P, N], U8, name="w_scales%d" % g, align_bytes=64))
             nc.scalar.copy(
-                w_bf[g].rearrange("p (c i) j -> p c j i", i=4),
+                w_bf[:, g * N : (g + 1) * N, :].rearrange("p (c i) j -> p c j i", i=4),
                 w_raw[g][:].rearrange("p j (c i) -> p c j i", i=4),
             )
-        gather(3, picked1, 0, S)
+        coef = sb.tile([P, 2, D], F32, name="coef")
+        total = sb.tile([P, 2], F32, name="total", tag="total", align_bytes=64)
+        stay = sb.tile([P, 2], F32, name="stay", tag="w_raw1", align_bytes=64)
+        gate_bank = ps.tile([P, 2, P], F32, name="gate_bank", tag="acc%d" % PIECES[-1][0])
+        for h in range(2):
+            nc.tensor.transpose(gate_bank[:, h, :], gate_rows[:, h * P : (h + 1) * P], eye[:])
+        for h in range(2):
+            nc.scalar.activation(coef[:, h, :], gate_bank[:, h, 0:D], ACT.Copy, accum_out=total[:, h : h + 1])
+        nc.scalar.activation(stay[:], total[:], ACT.Copy, scale=-1.0, bias=1.0)
+
+        gather_plain(3, words1, 0, S)
         for g in range(PASSES):
-            quantise(w_codes[g][:], w_scales[g], w_bf[g])
-        codes1 = sb.tile([P, S], U32, name="codes1", tag="w_raw1", align_bytes=64)
+            quantise(w_codes[:, g * N : (g + 1) * N], w_scales[:, g * N : (g + 1) * N], w_bf[:, g * N : (g + 1) * N, :])
+        picked1 = sb.tile([P, S, 4], BF16, name="picked1", tag="total", align_bytes=64)
+        for a, b in ((0, 256), (256, 512)):
+            weave(words1, picked1, a, b)
+        codes1 = sb.tile([P, S], U32, name="codes1", align_bytes=64)
 
         y = sb.tile([P, S], F32, name="y")
         acc = [ps.tile([P, b - a], F32, name="acc%d" % a, tag="acc%d" % a) for a, b in PIECES]
         for i, (a, b) in enumerate(PIECES):
-            nc.tensor.matmul_mx(out=acc[i][:], lhsT=w_codes[0][:].bitcast(FP8X4), lhsT_scale=w_scales[0][:],
+            nc.tensor.matmul_mx(out=acc[i][:], lhsT=w_codes[:, :N].bitcast(FP8X4), lhsT_scale=w_scales[:, :N],
                                 rhs=codes0[:, a:b].bitcast(FP8X4), rhs_scale=scales0[:, a:b], start=True, stop=False)
         for i, (a, b) in enumerate(PIECES):
-            quantise(codes1[:, a:b], scales1[i], picked1[:, a:b, :])
-            nc.tensor.matmul_mx(out=acc[i][:], lhsT=w_codes[1][:].bitcast(FP8X4), lhsT_scale=w_scales[1][:],
-                                rhs=codes1[:, a:b].bitcast(FP8X4), rhs_scale=scales1[i][:], start=False, stop=True)
+            quantise(codes1[:, a:b], scales1[:, a:b], picked1[:, a:b, :])
+            nc.tensor.matmul_mx(out=acc[i][:], lhsT=w_codes[:, N:].bitcast(FP8X4), lhsT_scale=w_scales[:, N:],
+                                rhs=codes1[:, a:b].bitcast(FP8X4), rhs_scale=scales1[:, a:b], start=False, stop=True)
             nc.scalar.activation(y[:, a:b], acc[i][:], ACT.Relu)
 
-        coef = sb.tile([P, 2, D], F32, name="coef")
-        total = sb.tile([P, 2], F32, name="total")
-        stay = sb.tile([P, 2], F32, name="stay")
-        bank = ps.tile([P, 2, P], F32, name="gate_bank", tag="acc%d" % PIECES[-1][0])
-        for h in range(2):
-            nc.tensor.transpose(bank[:, h, :], gate_rows[:, h * P : (h + 1) * P], eye[:])
-        for h in range(2):
-            nc.scalar.activation(coef[:, h, :], bank[:, h, 0:P:32], ACT.Copy, accum_out=total[:, h : h + 1])
-        nc.scalar.activation(stay[:], total[:], ACT.Copy, scale=-1.0, bias=1.0)
-
         sums = [ps.tile([P, P], F32, name="sums%d" % h) for h in range(2)]
-
-        banks = []
+        turned = {}
         for i in range(TURNED):
             fetched = sb.tile([P, V], F32, name="fetched%d" % i)
             nc.vector.tensor_copy(fetched[:], y[:].indirect(lists[i][:]))
-            banks.append(turn.tile([P, 2, P], F32, name="bank"))
+            if i < TURNED - 1:
+                bank = ps.tile([P, 2, P], F32, name="bank%d" % i)
+                halves = [bank[:, h, :] for h in range(2)]
+            else:
+                halves = [ps.tile([P, P], F32, name="bank_last%d" % h, tag="acc0" if h else "bank_last")[:] for h in range(2)]
             for h in range(2):
-                nc.tensor.transpose(banks[i][:, h, :], fetched[:, h * P : (h + 1) * P], eye[:])
+                nc.tensor.transpose(halves[h], fetched[:, h * P : (h + 1) * P], eye[:])
+                turned[i, h] = halves[h]
         for i in range(TURNED):
             for h in range(2):
                 scaled = sb.tile([P, P], F32, name="scaled%d_%d" % (i, h))
                 factor = stay[:, h : h + 1] if i == 0 else coef[:, h, i - 1 : i]
-                nc.scalar.activation(scaled[:], banks[i][:, h, :], ACT.Copy, scale=factor)
+                nc.scalar.activation(scaled[:], turned[i, h], ACT.Copy, scale=factor)
                 nc.tensor.matmul(sums[h][:], scaled[:], eye[:], start=(i == 0), stop=(i == TURNED - 1), is_transpose=True)
         terms = []
         for i in range(TURNED, D + 1):
             terms.append(sb.tile([P, V], F32, name="term%d" % i))
             nc.vector.tensor_tensor(terms[-1][:], y[:].indirect(lists[i][:]), gate_full[i][:], ALU.mult)
-        rest = terms[0]
-        for i, term in enumerate(terms[1:]):
-            both = sb.tile([P, V], F32, name="both%d" % i)
-            nc.vector.tensor_tensor(both[:], rest[:], term[:], ALU.add)
-            rest = both
+        both = sb.tile([P, V], F32, name="both")
+        nc.vector.tensor_tensor(both[:], terms[0][:], terms[1][:], ALU.add)
         for h in range(2):
             res = sb.tile([P, P], F32, name="res%d" % h)
-            nc.vector.tensor_tensor(res[:], sums[h][:], rest[:, h * P : (h + 1) * P], ALU.add)
+            nc.vector.tensor_tensor(res[:], sums[h][:], both[:, h * P : (h + 1) * P], ALU.add)
             nc.sync.dma_start(out=out[:, h * P : (h + 1) * P], in_=res[:])

@@ -23,7 +23,7 @@ TURNED = 3
 CHUNKS = (
     ((0, 512, 512), (512, 1024, 384)),
     ((0, 512, 0), (512, 1024, 384)),
-    ((0, 512, 0), (512, 1024, 128)),
+    ((0, 512, 0), (512, 1024, 0)),
     ((0, 512, 0), (512, 768, 0), (768, 1024, 256)),
 )
 
@@ -66,8 +66,7 @@ def tile_picked_grand_relu_e_kernel(tc, xT, w1, gate, offs, cen, pos1, pos2, pos
 
         pairs = [sb.tile([P, T, 2], BF16, name="pairs%d" % q, align_bytes=64) for q in range(4)]
         picked0 = sb.tile([P, S, 4], BF16, name="picked0", align_bytes=64)
-        words1 = sb.tile([P, 2, S], U32, name="words1")
-        words0 = sb.tile([P, 2, S], U32, name="words0")
+        words = [[sb.tile([P, 2, S // 2], U32, name="words%d_%d" % (g, h)) for h in range(2)] for g in range(PASSES)]
         codes0 = sb.tile([P, S], U32, name="codes0", align_bytes=64)
         scales0 = sb.tile([P, S], U8, name="scales0", align_bytes=64)
         scales1 = sb.tile([P, S], U8, name="scales1", align_bytes=64)
@@ -84,28 +83,32 @@ def tile_picked_grand_relu_e_kernel(tc, xT, w1, gate, offs, cen, pos1, pos2, pos
         def window(q):
             return pairs[q][:].rearrange("p t e -> p (t e)").bitcast(U32)
 
-        def gather(q, dst):
-            words = dst[:].rearrange("p n j -> p (n j)").bitcast(U32).rearrange("p (n u) -> p n u", u=2)
-            nc.vector.tensor_copy(words[:, :, q % 2], window(q).indirect(offs_sb[:]))
+        def gather(q):
+            for h in range(2):
+                nc.vector.tensor_copy(words[q // 2][h][:, q % 2, :], window(q).indirect(offs_sb[:, 16 * h : 16 * h + 16]))
 
-        def gather_plain(q, words, a, b):
-            nc.vector.tensor_copy(words[:, q % 2, a:b], window(q).indirect(offs_sb[:, a // 16 : b // 16]))
-
-        def weave(words, dst, a, b):
-            woven = dst[:, a:b, :].rearrange("p n j -> p (n j)").bitcast(I32).rearrange("p (n u) -> p n u", u=2)
-            nc.vector.tensor_copy(woven, words[:, :, a:b].bitcast(I32).rearrange("p u n -> p n u"))
+        def weave(g, h, dst, on_scalar):
+            dtype = U32 if on_scalar else I32
+            woven = dst[:, 256 * h : 256 * h + 256, :].rearrange("p n j -> p (n j)").bitcast(dtype).rearrange("p (n u) -> p n u", u=2)
+            src = words[g][h][:].bitcast(dtype).rearrange("p u n -> p n u")
+            if on_scalar:
+                nc.scalar.copy(woven, src)
+            else:
+                nc.vector.tensor_copy(woven, src)
 
         def quantise(codes, scales, src):
             nc.vector.quantize_mx(out=codes.bitcast(FP8X4), scales=scales, in_=src.rearrange("p n j -> p (n j)"))
 
         cast(0)
-        gather_plain(0, words0, 0, S)
+        gather(0)
         cast(1)
-        gather_plain(1, words0, 0, S)
-        weave(words0, picked0, 0, S)
+        gather(1)
+        for h in range(2):
+            weave(0, h, picked0, False)
+        for a, b in ((0, 256), (256, 512)):
+            quantise(codes0[:, a:b], scales0[:, a:b], picked0[:, a:b, :])
         cast(2)
-        quantise(codes0[:], scales0[:], picked0[:])
-        gather_plain(2, words1, 0, S)
+        gather(2)
         cast(3)
 
         w_bf = sb.tile([P, PASSES * N, 4], BF16, name="w_bf", tag="raw3_1", align_bytes=64)
@@ -117,8 +120,8 @@ def tile_picked_grand_relu_e_kernel(tc, xT, w1, gate, offs, cen, pos1, pos2, pos
                 w_raw[g][:].rearrange("p j (c i) -> p c j i", i=4),
             )
         coef = sb.tile([P, 2, D], F32, name="coef")
-        total = sb.tile([P, 2], F32, name="total", tag="total", align_bytes=64)
-        stay = sb.tile([P, 2], F32, name="stay", tag="w_raw1", align_bytes=64)
+        total = sb.tile([P, 2], F32, name="total")
+        stay = sb.tile([P, 2], F32, name="stay")
         gate_bank = ps.tile([P, 2, P], F32, name="gate_bank", tag="acc%d" % PIECES[-1][0])
         for h in range(2):
             nc.tensor.transpose(gate_bank[:, h, :], gate_rows[:, h * P : (h + 1) * P], eye[:])
@@ -126,12 +129,12 @@ def tile_picked_grand_relu_e_kernel(tc, xT, w1, gate, offs, cen, pos1, pos2, pos
             nc.scalar.activation(coef[:, h, :], gate_bank[:, h, 0:D], ACT.Copy, accum_out=total[:, h : h + 1])
         nc.scalar.activation(stay[:], total[:], ACT.Copy, scale=-1.0, bias=1.0)
 
-        gather_plain(3, words1, 0, S)
+        gather(3)
         for g in range(PASSES):
             quantise(w_codes[:, g * N : (g + 1) * N], w_scales[:, g * N : (g + 1) * N], w_bf[:, g * N : (g + 1) * N, :])
-        picked1 = sb.tile([P, S, 4], BF16, name="picked1", tag="total", align_bytes=64)
-        for a, b in ((0, 256), (256, 512)):
-            weave(words1, picked1, a, b)
+        picked1 = sb.tile([P, S, 4], BF16, name="picked1", tag="w_raw0", align_bytes=64)
+        for h in range(2):
+            weave(1, h, picked1, h == 1)
         codes1 = sb.tile([P, S], U32, name="codes1", align_bytes=64)
 
         y = sb.tile([P, S], F32, name="y")
@@ -164,13 +167,15 @@ def tile_picked_grand_relu_e_kernel(tc, xT, w1, gate, offs, cen, pos1, pos2, pos
                 factor = stay[:, h : h + 1] if i == 0 else coef[:, h, i - 1 : i]
                 nc.scalar.activation(scaled[:], turned[i, h], ACT.Copy, scale=factor)
                 nc.tensor.matmul(sums[h][:], scaled[:], eye[:], start=(i == 0), stop=(i == TURNED - 1), is_transpose=True)
-        terms = []
-        for i in range(TURNED, D + 1):
-            terms.append(sb.tile([P, V], F32, name="term%d" % i))
-            nc.vector.tensor_tensor(terms[-1][:], y[:].indirect(lists[i][:]), gate_full[i][:], ALU.mult)
-        both = sb.tile([P, V], F32, name="both")
-        nc.vector.tensor_tensor(both[:], terms[0][:], terms[1][:], ALU.add)
+        term3 = sb.tile([P, V], F32, name="term3")
+        nc.vector.tensor_tensor(term3[:], y[:].indirect(lists[3][:]), gate_full[3][:], ALU.mult)
+        term4 = [sb.tile([P, P], F32, name="term4_%d" % h) for h in range(2)]
+        both = [sb.tile([P, P], F32, name="both%d" % h) for h in range(2)]
+        for h in range(2):
+            nc.vector.tensor_tensor(term4[h][:], y[:].indirect(lists[4][:, 8 * h : 8 * h + 8]), gate_full[4][:, h * P : (h + 1) * P], ALU.mult)
+        for h in range(2):
+            nc.vector.tensor_tensor(both[h][:], term3[:, h * P : (h + 1) * P], term4[h][:], ALU.add)
         for h in range(2):
             res = sb.tile([P, P], F32, name="res%d" % h)
-            nc.vector.tensor_tensor(res[:], sums[h][:], both[:, h * P : (h + 1) * P], ALU.add)
+            nc.vector.tensor_tensor(res[:], sums[h][:], both[h][:], ALU.add)
             nc.sync.dma_start(out=out[:, h * P : (h + 1) * P], in_=res[:])

@@ -17,12 +17,15 @@ ACT = mybir.ActivationFunctionType
 ALU = mybir.AluOpType
 
 P = 128
+GROUP = 16
 PASSES = K // (4 * P)
+PLANES = 2 * PASSES
+HALF = S // 2
 PIECES = ((0, 256), (256, 384), (384, 512))
 TURNED = 3
 CHUNKS = (
-    ((0, 512, 512), (512, 1024, 384)),
-    ((0, 512, 0), (512, 1024, 384)),
+    ((0, 1024, 640),),
+    ((0, 1024, 640),),
     ((0, 512, 0), (512, 1024, 0)),
     ((0, 512, 0), (512, 768, 0), (768, 1024, 256)),
 )
@@ -37,12 +40,12 @@ def tile_picked_grand_relu_e_kernel(tc, xT, w1, gate, offs, cen, pos1, pos2, pos
         x_rows = xT.rearrange("(g p u e) t -> g u p e t", p=P, u=2, e=2)
         w_rows = w1.rearrange("(g p j) m -> g p j m", p=P, j=4)
 
-        offs_sb = sb.tile([P, S // 16], U16, name="offs_sb")
+        offs_sb = sb.tile([P, S // GROUP], U16, name="offs_sb")
         gate_rows = sb.tile([P, V], F32, name="gate_rows")
         nc.gpsimd.memset(gate_rows[:], 0.0)
         raw = {}
-        for q in range(4):
-            for c, (a, b, vshare) in enumerate(CHUNKS[q]):
+        for q in range(PLANES):
+            for c, (a, b, on_vector) in enumerate(CHUNKS[q]):
                 raw[q, c] = sb.tile([P, 2, b - a], F32, name="raw%d_%d" % (q, c), tag="raw%d_%d" % (q, c), align_bytes=64)
                 nc.sync.dma_start(out=raw[q, c][:], in_=x_rows[q // 2, q % 2, :, :, a:b])
                 if q == 0 and c == 0:
@@ -54,7 +57,7 @@ def tile_picked_grand_relu_e_kernel(tc, xT, w1, gate, offs, cen, pos1, pos2, pos
             nc.sync.dma_start(out=w_raw[g][:], in_=w_rows[g])
         lists = []
         for i, src in enumerate((cen, pos1, pos2, pos3, pos4)):
-            lists.append(sb.tile([P, V // 16], U16, name="list%d" % i))
+            lists.append(sb.tile([P, V // GROUP], U16, name="list%d" % i))
             nc.sync.dma_start(lists[i][:], src)
         gate_full = {}
         for i in range(TURNED, D + 1):
@@ -64,40 +67,41 @@ def tile_picked_grand_relu_e_kernel(tc, xT, w1, gate, offs, cen, pos1, pos2, pos
         eye = sb.tile([P, P], F32, name="eye")
         make_identity(nc, eye[:])
 
-        pairs = [sb.tile([P, T, 2], BF16, name="pairs%d" % q, align_bytes=64) for q in range(4)]
+        pairs = [sb.tile([P, T, 2], BF16, name="pairs%d" % q, align_bytes=64) for q in range(PLANES)]
         picked0 = sb.tile([P, S, 4], BF16, name="picked0", align_bytes=64)
-        words = [[sb.tile([P, 2, S // 2], U32, name="words%d_%d" % (g, h)) for h in range(2)] for g in range(PASSES)]
+        words = [[sb.tile([P, 2, HALF], U32, name="words%d_%d" % (g, h)) for h in range(2)] for g in range(PASSES)]
         codes0 = sb.tile([P, S], U32, name="codes0", align_bytes=64)
         scales0 = sb.tile([P, S], U8, name="scales0", align_bytes=64)
         scales1 = sb.tile([P, S], U8, name="scales1", align_bytes=64)
 
         def cast(q):
-            for c, (a, b, vshare) in enumerate(CHUNKS[q]):
+            for c, (a, b, on_vector) in enumerate(CHUNKS[q]):
                 src = raw[q, c][:].rearrange("p e t -> p t e")
-                split = b - a - vshare
-                if split:
-                    nc.scalar.activation(pairs[q][:, a : a + split, :], src[:, :split, :], ACT.Copy)
-                if vshare:
-                    nc.vector.tensor_copy(pairs[q][:, a + split : b, :], src[:, split:, :])
-
-        def window(q):
-            return pairs[q][:].rearrange("p t e -> p (t e)").bitcast(U32)
+                on_scalar = b - a - on_vector
+                if on_scalar:
+                    nc.scalar.activation(pairs[q][:, a : a + on_scalar, :], src[:, :on_scalar, :], ACT.Copy)
+                if on_vector:
+                    nc.vector.tensor_copy(pairs[q][:, a + on_scalar : b, :], src[:, on_scalar:, :])
 
         def gather(q):
+            window = pairs[q][:].rearrange("p t e -> p (t e)").bitcast(U32)
+            columns = HALF // GROUP
             for h in range(2):
-                nc.vector.tensor_copy(words[q // 2][h][:, q % 2, :], window(q).indirect(offs_sb[:, 16 * h : 16 * h + 16]))
+                offsets = offs_sb[:, columns * h : columns * (h + 1)]
+                nc.vector.tensor_copy(words[q // 2][h][:, q % 2, :], window.indirect(offsets))
 
-        def weave(g, h, dst, on_scalar):
+        def weave(g, h, picked, on_scalar):
             dtype = U32 if on_scalar else I32
-            woven = dst[:, 256 * h : 256 * h + 256, :].rearrange("p n j -> p (n j)").bitcast(dtype).rearrange("p (n u) -> p n u", u=2)
+            groups = picked[:, HALF * h : HALF * (h + 1), :].rearrange("p n j -> p (n j)")
+            woven = groups.bitcast(dtype).rearrange("p (n u) -> p n u", u=2)
             src = words[g][h][:].bitcast(dtype).rearrange("p u n -> p n u")
             if on_scalar:
                 nc.scalar.copy(woven, src)
             else:
                 nc.vector.tensor_copy(woven, src)
 
-        def quantise(codes, scales, src):
-            nc.vector.quantize_mx(out=codes.bitcast(FP8X4), scales=scales, in_=src.rearrange("p n j -> p (n j)"))
+        def quantise(codes, scales, groups):
+            nc.vector.quantize_mx(out=codes.bitcast(FP8X4), scales=scales, in_=groups.rearrange("p n j -> p (n j)"))
 
         cast(0)
         gather(0)
@@ -105,8 +109,9 @@ def tile_picked_grand_relu_e_kernel(tc, xT, w1, gate, offs, cen, pos1, pos2, pos
         gather(1)
         for h in range(2):
             weave(0, h, picked0, False)
-        for a, b in ((0, 256), (256, 512)):
-            quantise(codes0[:, a:b], scales0[:, a:b], picked0[:, a:b, :])
+        for h in range(2):
+            nodes = slice(HALF * h, HALF * (h + 1))
+            quantise(codes0[:, nodes], scales0[:, nodes], picked0[:, nodes, :])
         cast(2)
         gather(2)
         cast(3)
@@ -119,6 +124,7 @@ def tile_picked_grand_relu_e_kernel(tc, xT, w1, gate, offs, cen, pos1, pos2, pos
                 w_bf[:, g * N : (g + 1) * N, :].rearrange("p (c i) j -> p c j i", i=4),
                 w_raw[g][:].rearrange("p j (c i) -> p c j i", i=4),
             )
+
         coef = sb.tile([P, 2, D], F32, name="coef")
         total = sb.tile([P, 2], F32, name="total")
         stay = sb.tile([P, 2], F32, name="stay")
@@ -131,7 +137,8 @@ def tile_picked_grand_relu_e_kernel(tc, xT, w1, gate, offs, cen, pos1, pos2, pos
 
         gather(3)
         for g in range(PASSES):
-            quantise(w_codes[:, g * N : (g + 1) * N], w_scales[:, g * N : (g + 1) * N], w_bf[:, g * N : (g + 1) * N, :])
+            cols = slice(g * N, (g + 1) * N)
+            quantise(w_codes[:, cols], w_scales[:, cols], w_bf[:, cols, :])
         picked1 = sb.tile([P, S, 4], BF16, name="picked1", tag="w_raw0", align_bytes=64)
         for h in range(2):
             weave(1, h, picked1, h == 1)
@@ -140,12 +147,26 @@ def tile_picked_grand_relu_e_kernel(tc, xT, w1, gate, offs, cen, pos1, pos2, pos
         y = sb.tile([P, S], F32, name="y")
         acc = [ps.tile([P, b - a], F32, name="acc%d" % a, tag="acc%d" % a) for a, b in PIECES]
         for i, (a, b) in enumerate(PIECES):
-            nc.tensor.matmul_mx(out=acc[i][:], lhsT=w_codes[:, :N].bitcast(FP8X4), lhsT_scale=w_scales[:, :N],
-                                rhs=codes0[:, a:b].bitcast(FP8X4), rhs_scale=scales0[:, a:b], start=True, stop=False)
+            nc.tensor.matmul_mx(
+                out=acc[i][:],
+                lhsT=w_codes[:, :N].bitcast(FP8X4),
+                lhsT_scale=w_scales[:, :N],
+                rhs=codes0[:, a:b].bitcast(FP8X4),
+                rhs_scale=scales0[:, a:b],
+                start=True,
+                stop=False,
+            )
         for i, (a, b) in enumerate(PIECES):
             quantise(codes1[:, a:b], scales1[:, a:b], picked1[:, a:b, :])
-            nc.tensor.matmul_mx(out=acc[i][:], lhsT=w_codes[:, N:].bitcast(FP8X4), lhsT_scale=w_scales[:, N:],
-                                rhs=codes1[:, a:b].bitcast(FP8X4), rhs_scale=scales1[:, a:b], start=False, stop=True)
+            nc.tensor.matmul_mx(
+                out=acc[i][:],
+                lhsT=w_codes[:, N:].bitcast(FP8X4),
+                lhsT_scale=w_scales[:, N:],
+                rhs=codes1[:, a:b].bitcast(FP8X4),
+                rhs_scale=scales1[:, a:b],
+                start=False,
+                stop=True,
+            )
             nc.scalar.activation(y[:, a:b], acc[i][:], ACT.Relu)
 
         sums = [ps.tile([P, P], F32, name="sums%d" % h) for h in range(2)]
@@ -155,24 +176,27 @@ def tile_picked_grand_relu_e_kernel(tc, xT, w1, gate, offs, cen, pos1, pos2, pos
             nc.vector.tensor_copy(fetched[:], y[:].indirect(lists[i][:]))
             if i < TURNED - 1:
                 bank = ps.tile([P, 2, P], F32, name="bank%d" % i)
-                halves = [bank[:, h, :] for h in range(2)]
+                targets = [bank[:, h, :] for h in range(2)]
             else:
-                halves = [ps.tile([P, P], F32, name="bank_last%d" % h, tag="acc0" if h else "bank_last")[:] for h in range(2)]
+                targets = [ps.tile([P, P], F32, name="bank_last%d" % h, tag="acc0" if h else "bank_last")[:] for h in range(2)]
             for h in range(2):
-                nc.tensor.transpose(halves[h], fetched[:, h * P : (h + 1) * P], eye[:])
-                turned[i, h] = halves[h]
+                nc.tensor.transpose(targets[h], fetched[:, h * P : (h + 1) * P], eye[:])
+                turned[i, h] = targets[h]
         for i in range(TURNED):
             for h in range(2):
                 scaled = sb.tile([P, P], F32, name="scaled%d_%d" % (i, h))
                 factor = stay[:, h : h + 1] if i == 0 else coef[:, h, i - 1 : i]
                 nc.scalar.activation(scaled[:], turned[i, h], ACT.Copy, scale=factor)
                 nc.tensor.matmul(sums[h][:], scaled[:], eye[:], start=(i == 0), stop=(i == TURNED - 1), is_transpose=True)
+
         term3 = sb.tile([P, V], F32, name="term3")
-        nc.vector.tensor_tensor(term3[:], y[:].indirect(lists[3][:]), gate_full[3][:], ALU.mult)
+        nc.vector.tensor_tensor(term3[:], y[:].indirect(lists[D - 1][:]), gate_full[D - 1][:], ALU.mult)
         term4 = [sb.tile([P, P], F32, name="term4_%d" % h) for h in range(2)]
         both = [sb.tile([P, P], F32, name="both%d" % h) for h in range(2)]
+        columns = P // GROUP
         for h in range(2):
-            nc.vector.tensor_tensor(term4[h][:], y[:].indirect(lists[4][:, 8 * h : 8 * h + 8]), gate_full[4][:, h * P : (h + 1) * P], ALU.mult)
+            offsets = lists[D][:, columns * h : columns * (h + 1)]
+            nc.vector.tensor_tensor(term4[h][:], y[:].indirect(offsets), gate_full[D][:, h * P : (h + 1) * P], ALU.mult)
         for h in range(2):
             nc.vector.tensor_tensor(both[h][:], term3[:, h * P : (h + 1) * P], term4[h][:], ALU.add)
         for h in range(2):

@@ -8,7 +8,6 @@ FLOPS = 2 * K * N * S
 
 F32 = mybir.dt.float32
 BF16 = mybir.dt.bfloat16
-I32 = mybir.dt.int32
 U32 = mybir.dt.uint32
 U16 = mybir.dt.uint16
 U8 = mybir.dt.uint8
@@ -24,10 +23,10 @@ HALF = S // 2
 PIECES = ((0, 256), (256, 384), (384, 512))
 TURNED = 3
 CHUNKS = (
-    ((0, 1024, 640),),
-    ((0, 1024, 640),),
-    ((0, 512, 0), (512, 1024, 0)),
-    ((0, 512, 0), (512, 768, 0), (768, 1024, 256)),
+    ((("vector", 512),), (("scalar", 160), ("vector", 352))),
+    ((("scalar", 512),), (("scalar", 160), ("vector", 352))),
+    ((("scalar", 256), ("gpsimd", 256)), (("vector", 512),)),
+    ((("scalar", 256), ("gpsimd", 256)), (("scalar", 192), ("gpsimd", 192)), (("scalar", 128),)),
 )
 
 
@@ -45,7 +44,9 @@ def tile_picked_grand_relu_e_kernel(tc, xT, w1, gate, offs, cen, pos1, pos2, pos
         nc.gpsimd.memset(gate_rows[:], 0.0)
         raw = {}
         for q in range(PLANES):
-            for c, (a, b, on_vector) in enumerate(CHUNKS[q]):
+            b = 0
+            for c, shares in enumerate(CHUNKS[q]):
+                a, b = b, b + sum(n for engine, n in shares)
                 raw[q, c] = sb.tile([P, 2, b - a], F32, name="raw%d_%d" % (q, c), tag="raw%d_%d" % (q, c), align_bytes=64)
                 nc.sync.dma_start(out=raw[q, c][:], in_=x_rows[q // 2, q % 2, :, :, a:b])
                 if q == 0 and c == 0:
@@ -68,62 +69,41 @@ def tile_picked_grand_relu_e_kernel(tc, xT, w1, gate, offs, cen, pos1, pos2, pos
         make_identity(nc, eye[:])
 
         pairs = [sb.tile([P, T, 2], BF16, name="pairs%d" % q, align_bytes=64) for q in range(PLANES)]
-        picked0 = sb.tile([P, S, 4], BF16, name="picked0", align_bytes=64)
-        words = [[sb.tile([P, 2, HALF], U32, name="words%d_%d" % (g, h)) for h in range(2)] for g in range(PASSES)]
-        codes0 = sb.tile([P, S], U32, name="codes0", align_bytes=64)
-        scales0 = sb.tile([P, S], U8, name="scales0", align_bytes=64)
-        scales1 = sb.tile([P, S], U8, name="scales1", align_bytes=64)
+        picked = {}
+        both_planes = [sb.tile([P, 2, S], U32, name="words%d" % g) for g in range(PASSES)]
+        words = [both_planes[q // 2][:, q % 2, :] for q in range(PLANES)]
+        codes = [sb.tile([P, S], U32, name="codes%d" % g, align_bytes=64) for g in range(PASSES)]
+        scales = [sb.tile([P, S], U8, name="scales%d" % g, align_bytes=64) for g in range(PASSES)]
+
+        def round_to_bf16(engine, dst, src):
+            if engine == "scalar":
+                nc.scalar.activation(dst, src, ACT.Copy)
+            elif engine == "vector":
+                nc.vector.tensor_copy(dst, src)
+            else:
+                nc.gpsimd.tensor_scalar(dst, src, 1.0, 0.0, ALU.mult, ALU.add)
 
         def cast(q):
-            for c, (a, b, on_vector) in enumerate(CHUNKS[q]):
+            first = 0
+            for c, shares in enumerate(CHUNKS[q]):
                 src = raw[q, c][:].rearrange("p e t -> p t e")
-                on_scalar = b - a - on_vector
-                if on_scalar:
-                    nc.scalar.activation(pairs[q][:, a : a + on_scalar, :], src[:, :on_scalar, :], ACT.Copy)
-                if on_vector:
-                    nc.vector.tensor_copy(pairs[q][:, a + on_scalar : b, :], src[:, on_scalar:, :])
+                a = 0
+                for engine, n in shares:
+                    round_to_bf16(engine, pairs[q][:, first + a : first + a + n, :], src[:, a : a + n, :])
+                    a += n
+                first += a
 
-        def gather(q):
+        def gather(q, a, b):
             window = pairs[q][:].rearrange("p t e -> p (t e)").bitcast(U32)
-            columns = HALF // GROUP
-            for h in range(2):
-                offsets = offs_sb[:, columns * h : columns * (h + 1)]
-                nc.vector.tensor_copy(words[q // 2][h][:, q % 2, :], window.indirect(offsets))
+            nc.vector.tensor_copy(words[q][:, a:b], window.indirect(offs_sb[:, a // GROUP : b // GROUP]))
 
-        def weave(g, h, picked, on_scalar):
-            dtype = U32 if on_scalar else I32
-            groups = picked[:, HALF * h : HALF * (h + 1), :].rearrange("p n j -> p (n j)")
-            woven = groups.bitcast(dtype).rearrange("p (n u) -> p n u", u=2)
-            src = words[g][h][:].bitcast(dtype).rearrange("p u n -> p n u")
-            if on_scalar:
-                nc.scalar.copy(woven, src)
-            else:
-                nc.vector.tensor_copy(woven, src)
+        def weave(g, a, b):
+            groups = picked[g][:, a:b, :].rearrange("p n j -> p (n j)")
+            woven = groups.bitcast(U32).rearrange("p (n u) -> p n u", u=2)
+            nc.scalar.copy(woven, both_planes[g][:, :, a:b].rearrange("p u n -> p n u"))
 
-        def quantise(codes, scales, groups):
-            nc.vector.quantize_mx(out=codes.bitcast(FP8X4), scales=scales, in_=groups.rearrange("p n j -> p (n j)"))
-
-        cast(0)
-        gather(0)
-        cast(1)
-        gather(1)
-        for h in range(2):
-            weave(0, h, picked0, False)
-        for h in range(2):
-            nodes = slice(HALF * h, HALF * (h + 1))
-            quantise(codes0[:, nodes], scales0[:, nodes], picked0[:, nodes, :])
-        cast(2)
-        gather(2)
-        cast(3)
-
-        w_bf = sb.tile([P, PASSES * N, 4], BF16, name="w_bf", tag="raw3_1", align_bytes=64)
-        w_codes = sb.tile([P, PASSES * N], U32, name="w_codes", align_bytes=64)
-        w_scales = sb.tile([P, PASSES * N], U8, name="w_scales", align_bytes=64)
-        for g in range(PASSES):
-            nc.scalar.copy(
-                w_bf[:, g * N : (g + 1) * N, :].rearrange("p (c i) j -> p c j i", i=4),
-                w_raw[g][:].rearrange("p j (c i) -> p c j i", i=4),
-            )
+        def quantise(packed, plane, groups):
+            nc.vector.quantize_mx(out=packed.bitcast(FP8X4), scales=plane, in_=groups.rearrange("p n j -> p (n j)"))
 
         coef = sb.tile([P, 2, D], F32, name="coef")
         total = sb.tile([P, 2], F32, name="total")
@@ -135,39 +115,63 @@ def tile_picked_grand_relu_e_kernel(tc, xT, w1, gate, offs, cen, pos1, pos2, pos
             nc.scalar.activation(coef[:, h, :], gate_bank[:, h, 0:D], ACT.Copy, accum_out=total[:, h : h + 1])
         nc.scalar.activation(stay[:], total[:], ACT.Copy, scale=-1.0, bias=1.0)
 
-        gather(3)
+        cast(0)
+        gather(0, 0, S)
+        cast(1)
+        for h in range(2):
+            gather(1, HALF * h, HALF * (h + 1))
+        cast(2)
+        picked[0] = sb.tile([P, S, 4], BF16, name="picked0", tag="raw2_0", align_bytes=64)
+        for h in range(2):
+            weave(0, HALF * h, HALF * (h + 1))
+        for h in range(2):
+            nodes = slice(HALF * h, HALF * (h + 1))
+            quantise(codes[0][:, nodes], scales[0][:, nodes], picked[0][:, nodes, :])
+        gather(2, 0, S)
+        cast(3)
+        for h in range(2):
+            gather(3, HALF * h, HALF * (h + 1))
+
+        w_bf = sb.tile([P, PASSES * N, 4], BF16, name="w_bf", tag="raw3_1", align_bytes=64)
+        w_codes = sb.tile([P, PASSES * N], U32, name="w_codes", align_bytes=64)
+        w_scales = sb.tile([P, PASSES * N], U8, name="w_scales", align_bytes=64)
+        for g in range(PASSES):
+            round_to_bf16(
+                "gpsimd" if g else "scalar",
+                w_bf[:, g * N : (g + 1) * N, :],
+                w_raw[g][:].rearrange("p j m -> p m j"),
+            )
         for g in range(PASSES):
             cols = slice(g * N, (g + 1) * N)
             quantise(w_codes[:, cols], w_scales[:, cols], w_bf[:, cols, :])
-        picked1 = sb.tile([P, S, 4], BF16, name="picked1", tag="w_raw0", align_bytes=64)
-        for h in range(2):
-            weave(1, h, picked1, h == 1)
-        codes1 = sb.tile([P, S], U32, name="codes1", align_bytes=64)
+        picked[1] = sb.tile([P, S, 4], BF16, name="picked1", tag="w_raw0", align_bytes=64)
+        for a, b in PIECES:
+            weave(1, a, b)
 
         y = sb.tile([P, S], F32, name="y")
         acc = [ps.tile([P, b - a], F32, name="acc%d" % a, tag="acc%d" % a) for a, b in PIECES]
-        for i, (a, b) in enumerate(PIECES):
+
+        def product(g, i):
+            a, b = PIECES[i]
             nc.tensor.matmul_mx(
                 out=acc[i][:],
-                lhsT=w_codes[:, :N].bitcast(FP8X4),
-                lhsT_scale=w_scales[:, :N],
-                rhs=codes0[:, a:b].bitcast(FP8X4),
-                rhs_scale=scales0[:, a:b],
-                start=True,
-                stop=False,
+                lhsT=w_codes[:, g * N : (g + 1) * N].bitcast(FP8X4),
+                lhsT_scale=w_scales[:, g * N : (g + 1) * N],
+                rhs=codes[g][:, a:b].bitcast(FP8X4),
+                rhs_scale=scales[g][:, a:b],
+                start=(g == 0),
+                stop=(g == PASSES - 1),
             )
+
+        for i in range(len(PIECES)):
+            product(0, i)
         for i, (a, b) in enumerate(PIECES):
-            quantise(codes1[:, a:b], scales1[:, a:b], picked1[:, a:b, :])
-            nc.tensor.matmul_mx(
-                out=acc[i][:],
-                lhsT=w_codes[:, N:].bitcast(FP8X4),
-                lhsT_scale=w_scales[:, N:],
-                rhs=codes1[:, a:b].bitcast(FP8X4),
-                rhs_scale=scales1[:, a:b],
-                start=False,
-                stop=True,
-            )
-            nc.scalar.activation(y[:, a:b], acc[i][:], ACT.Relu)
+            quantise(codes[1][:, a:b], scales[1][:, a:b], picked[1][:, a:b, :])
+            product(1, i)
+            if b < S:
+                nc.scalar.activation(y[:, a:b], acc[i][:], ACT.Relu)
+            else:
+                nc.vector.tensor_scalar_max(y[:, a:b], acc[i][:], 0.0)
 
         sums = [ps.tile([P, P], F32, name="sums%d" % h) for h in range(2)]
         turned = {}

@@ -23,8 +23,8 @@ HALF = S // 2
 PIECES = ((0, 256), (256, 384), (384, 512))
 TURNED = 3
 CHUNKS = (
-    ((("vector", 512),), (("scalar", 160), ("vector", 352))),
-    ((("scalar", 512),), (("scalar", 160), ("vector", 352))),
+    ((("scalar", 352), ("vector", 672)),),
+    ((("scalar", 352), ("vector", 672)),),
     ((("scalar", 256), ("gpsimd", 256)), (("vector", 512),)),
     ((("scalar", 256), ("gpsimd", 256)), (("scalar", 192), ("gpsimd", 192)), (("scalar", 128),)),
 )

@@ -99,8 +99,8 @@ def tile_picked_grand_relu_e_kernel(tc, xT, w1, gate, offs, cen, pos1, pos2, pos
 
         def weave(g, a, b):
             groups = picked[g][:, a:b, :].rearrange("p n j -> p (n j)")
-            woven = groups.bitcast(U32).rearrange("p (n u) -> p n u", u=2)
-            nc.scalar.copy(woven, both_planes[g][:, :, a:b].rearrange("p u n -> p n u"))
+            woven = groups.bitcast(U32).rearrange("p (c i u) -> p c u i", i=4, u=2)
+            nc.scalar.copy(woven, both_planes[g][:, :, a:b].rearrange("p u (c i) -> p c u i", i=4))
 
         def quantise(packed, plane, groups):
             nc.vector.quantize_mx(out=packed.bitcast(FP8X4), scales=plane, in_=groups.rearrange("p n j -> p (n j)"))
@@ -129,8 +129,8 @@ def tile_picked_grand_relu_e_kernel(tc, xT, w1, gate, offs, cen, pos1, pos2, pos
             quantise(codes[0][:, nodes], scales[0][:, nodes], picked[0][:, nodes, :])
         gather(2, 0, S)
         cast(3)
-        for h in range(2):
-            gather(3, HALF * h, HALF * (h + 1))
+        for a, b in PIECES:
+            gather(3, a, b)
 
         w_bf = sb.tile([P, PASSES * N, 4], BF16, name="w_bf", tag="raw3_1", align_bytes=64)
         w_codes = sb.tile([P, PASSES * N], U32, name="w_codes", align_bytes=64)
@@ -168,7 +168,7 @@ def tile_picked_grand_relu_e_kernel(tc, xT, w1, gate, offs, cen, pos1, pos2, pos
         for i, (a, b) in enumerate(PIECES):
             quantise(codes[1][:, a:b], scales[1][:, a:b], picked[1][:, a:b, :])
             product(1, i)
-            if b < S:
+            if i != 1:
                 nc.scalar.activation(y[:, a:b], acc[i][:], ACT.Relu)
             else:
                 nc.vector.tensor_scalar_max(y[:, a:b], acc[i][:], 0.0)

@@ -26,7 +26,7 @@ CHUNKS = (
     ((("scalar", 352), ("vector", 672)),),
     ((("scalar", 352), ("vector", 672)),),
     ((("scalar", 256), ("gpsimd", 256)), (("vector", 512),)),
-    ((("scalar", 256), ("gpsimd", 256)), (("scalar", 192), ("gpsimd", 192)), (("scalar", 128),)),
+    ((("scalar", 384), ("gpsimd", 256)), (("scalar", 128), ("vector", 256))),
 )
 
 
@@ -174,14 +174,18 @@ def tile_picked_grand_relu_e_kernel(tc, xT, w1, gate, offs, cen, pos1, pos2, pos
                 nc.vector.tensor_scalar_max(y[:, a:b], acc[i][:], 0.0)
 
         sums = [ps.tile([P, P], F32, name="sums%d" % h) for h in range(2)]
+        columns = P // GROUP
         turned = {}
         for i in range(TURNED):
             fetched = sb.tile([P, V], F32, name="fetched%d" % i)
-            nc.vector.tensor_copy(fetched[:], y[:].indirect(lists[i][:]))
             if i < TURNED - 1:
+                nc.vector.tensor_copy(fetched[:], y[:].indirect(lists[i][:]))
                 bank = ps.tile([P, 2, P], F32, name="bank%d" % i)
                 targets = [bank[:, h, :] for h in range(2)]
             else:
+                for h in range(2):
+                    offsets = lists[i][:, columns * h : columns * (h + 1)]
+                    nc.vector.tensor_copy(fetched[:, h * P : (h + 1) * P], y[:].indirect(offsets))
                 targets = [ps.tile([P, P], F32, name="bank_last%d" % h, tag="acc0" if h else "bank_last")[:] for h in range(2)]
             for h in range(2):
                 nc.tensor.transpose(targets[h], fetched[:, h * P : (h + 1) * P], eye[:])
@@ -197,7 +201,6 @@ def tile_picked_grand_relu_e_kernel(tc, xT, w1, gate, offs, cen, pos1, pos2, pos
         nc.vector.tensor_tensor(term3[:], y[:].indirect(lists[D - 1][:]), gate_full[D - 1][:], ALU.mult)
         term4 = [sb.tile([P, P], F32, name="term4_%d" % h) for h in range(2)]
         both = [sb.tile([P, P], F32, name="both%d" % h) for h in range(2)]
-        columns = P // GROUP
         for h in range(2):
             offsets = lists[D][:, columns * h : columns * (h + 1)]
             nc.vector.tensor_tensor(term4[h][:], y[:].indirect(offsets), gate_full[D][:, h * P : (h + 1) * P], ALU.mult)

@@ -25,8 +25,8 @@ TURNED = 3
 CHUNKS = (
     ((("scalar", 352), ("vector", 672)),),
     ((("scalar", 352), ("vector", 672)),),
-    ((("scalar", 256), ("gpsimd", 256)), (("vector", 512),)),
-    ((("scalar", 384), ("gpsimd", 256)), (("scalar", 128), ("vector", 256))),
+    ((("scalar", 256), ("gpsimd", 256)), (("scalar", 128), ("vector", 384))),
+    ((("scalar", 384), ("gpsimd", 256)), (("scalar", 192), ("vector", 192))),
 )
 
 
@@ -34,6 +34,7 @@ def tile_picked_grand_relu_e_kernel(tc, xT, w1, gate, offs, cen, pos1, pos2, pos
     nc = tc.nc
     with ExitStack() as ctx:
         sb = ctx.enter_context(tc.tile_pool(name="sb", bufs=1))
+        shared = ctx.enter_context(tc.tile_pool(name="shared", bufs=1))
         ps = ctx.enter_context(tc.psum_pool(name="ps", bufs=1))
 
         x_rows = xT.rearrange("(g p u e) t -> g u p e t", p=P, u=2, e=2)
@@ -47,7 +48,10 @@ def tile_picked_grand_relu_e_kernel(tc, xT, w1, gate, offs, cen, pos1, pos2, pos
             b = 0
             for c, shares in enumerate(CHUNKS[q]):
                 a, b = b, b + sum(n for engine, n in shares)
-                raw[q, c] = sb.tile([P, 2, b - a], F32, name="raw%d_%d" % (q, c), tag="raw%d_%d" % (q, c), align_bytes=64)
+                if b == T and q == PLANES - 1:
+                    raw[q, c] = shared.tile([P, 2, b - a], F32, name="raw_last", offset=0, align_bytes=64)
+                else:
+                    raw[q, c] = sb.tile([P, 2, b - a], F32, name="raw%d_%d" % (q, c), tag="raw%d_%d" % (q, c), align_bytes=64)
                 nc.sync.dma_start(out=raw[q, c][:], in_=x_rows[q // 2, q % 2, :, :, a:b])
                 if q == 0 and c == 0:
                     nc.sync.dma_start(offs_sb[:], offs)
@@ -69,10 +73,8 @@ def tile_picked_grand_relu_e_kernel(tc, xT, w1, gate, offs, cen, pos1, pos2, pos
         make_identity(nc, eye[:])
 
         pairs = [sb.tile([P, T, 2], BF16, name="pairs%d" % q, align_bytes=64) for q in range(PLANES)]
-        picked = {}
         both_planes = [sb.tile([P, 2, S], U32, name="words%d" % g) for g in range(PASSES)]
         words = [both_planes[q // 2][:, q % 2, :] for q in range(PLANES)]
-        codes = [sb.tile([P, S], U32, name="codes%d" % g, align_bytes=64) for g in range(PASSES)]
         scales = [sb.tile([P, S], U8, name="scales%d" % g, align_bytes=64) for g in range(PASSES)]
 
         def round_to_bf16(engine, dst, src):
@@ -97,9 +99,8 @@ def tile_picked_grand_relu_e_kernel(tc, xT, w1, gate, offs, cen, pos1, pos2, pos
             window = pairs[q][:].rearrange("p t e -> p (t e)").bitcast(U32)
             nc.vector.tensor_copy(words[q][:, a:b], window.indirect(offs_sb[:, a // GROUP : b // GROUP]))
 
-        def weave(g, a, b):
-            groups = picked[g][:, a:b, :].rearrange("p n j -> p (n j)")
-            woven = groups.bitcast(U32).rearrange("p (c i u) -> p c u i", i=4, u=2)
+        def weave(groups, g, a, b):
+            woven = groups.rearrange("p n j -> p (n j)").bitcast(U32).rearrange("p (c i u) -> p c u i", i=4, u=2)
             nc.scalar.copy(woven, both_planes[g][:, :, a:b].rearrange("p u (c i) -> p c u i", i=4))
 
         def quantise(packed, plane, groups):
@@ -121,18 +122,20 @@ def tile_picked_grand_relu_e_kernel(tc, xT, w1, gate, offs, cen, pos1, pos2, pos
         for h in range(2):
             gather(1, HALF * h, HALF * (h + 1))
         cast(2)
-        picked[0] = sb.tile([P, S, 4], BF16, name="picked0", tag="raw2_0", align_bytes=64)
+        picked0 = [sb.tile([P, HALF, 4], BF16, name="picked0_%d" % h, tag="raw2_%d" % h, align_bytes=64) for h in range(2)]
         for h in range(2):
-            weave(0, HALF * h, HALF * (h + 1))
-        for h in range(2):
-            nodes = slice(HALF * h, HALF * (h + 1))
-            quantise(codes[0][:, nodes], scales[0][:, nodes], picked[0][:, nodes, :])
+            weave(picked0[h][:], 0, HALF * h, HALF * (h + 1))
+        codes0 = [sb.tile([P, HALF], U32, name="codes0_0", align_bytes=64)]
+        quantise(codes0[0][:], scales[0][:, :HALF], picked0[0][:])
         gather(2, 0, S)
+        codes0.append(sb.tile([P, HALF], U32, name="codes0_1", align_bytes=64))
+        quantise(codes0[1][:], scales[0][:, HALF:], picked0[1][:])
         cast(3)
+        codes1 = sb.tile([P, S], U32, name="codes1", align_bytes=64)
         for a, b in PIECES:
             gather(3, a, b)
 
-        w_bf = sb.tile([P, PASSES * N, 4], BF16, name="w_bf", tag="raw3_1", align_bytes=64)
+        w_bf = shared.tile([P, PASSES * N, 4], BF16, name="w_bf", offset=4 * HALF, align_bytes=64)
         w_codes = sb.tile([P, PASSES * N], U32, name="w_codes", align_bytes=64)
         w_scales = sb.tile([P, PASSES * N], U8, name="w_scales", align_bytes=64)
         for g in range(PASSES):
@@ -144,20 +147,21 @@ def tile_picked_grand_relu_e_kernel(tc, xT, w1, gate, offs, cen, pos1, pos2, pos
         for g in range(PASSES):
             cols = slice(g * N, (g + 1) * N)
             quantise(w_codes[:, cols], w_scales[:, cols], w_bf[:, cols, :])
-        picked[1] = sb.tile([P, S, 4], BF16, name="picked1", tag="w_raw0", align_bytes=64)
+        picked1 = sb.tile([P, S, 4], BF16, name="picked1", tag="w_raw0", align_bytes=64)
         for a, b in PIECES:
-            weave(1, a, b)
+            weave(picked1[:, a:b, :], 1, a, b)
 
         y = sb.tile([P, S], F32, name="y")
         acc = [ps.tile([P, b - a], F32, name="acc%d" % a, tag="acc%d" % a) for a, b in PIECES]
 
         def product(g, i):
             a, b = PIECES[i]
+            codes = codes1[:, a:b] if g else codes0[a // HALF][:, a % HALF : a % HALF + b - a]
             nc.tensor.matmul_mx(
                 out=acc[i][:],
                 lhsT=w_codes[:, g * N : (g + 1) * N].bitcast(FP8X4),
                 lhsT_scale=w_scales[:, g * N : (g + 1) * N],
-                rhs=codes[g][:, a:b].bitcast(FP8X4),
+                rhs=codes.bitcast(FP8X4),
                 rhs_scale=scales[g][:, a:b],
                 start=(g == 0),
                 stop=(g == PASSES - 1),
@@ -166,7 +170,7 @@ def tile_picked_grand_relu_e_kernel(tc, xT, w1, gate, offs, cen, pos1, pos2, pos
         for i in range(len(PIECES)):
             product(0, i)
         for i, (a, b) in enumerate(PIECES):
-            quantise(codes[1][:, a:b], scales[1][:, a:b], picked[1][:, a:b, :])
+            quantise(codes1[:, a:b], scales[1][:, a:b], picked1[:, a:b, :])
             product(1, i)
             if i != 1:
                 nc.scalar.activation(y[:, a:b], acc[i][:], ACT.Relu)

@@ -21,7 +21,7 @@ PASSES = K // (4 * P)
 PLANES = 2 * PASSES
 HALF = S // 2
 PIECES = ((0, 256), (256, 384), (384, 512))
-TURNED = 3
+TURNED = 2
 CHUNKS = (
     ((("scalar", 352), ("vector", 672)),),
     ((("scalar", 352), ("vector", 672)),),
@@ -180,37 +180,36 @@ def tile_picked_grand_relu_e_kernel(tc, xT, w1, gate, offs, cen, pos1, pos2, pos
         sums = [ps.tile([P, P], F32, name="sums%d" % h) for h in range(2)]
         columns = P // GROUP
         turned = {}
-        for i in range(TURNED):
-            fetched = sb.tile([P, V], F32, name="fetched%d" % i)
-            if i < TURNED - 1:
-                nc.vector.tensor_copy(fetched[:], y[:].indirect(lists[i][:]))
-                bank = ps.tile([P, 2, P], F32, name="bank%d" % i)
-                targets = [bank[:, h, :] for h in range(2)]
-            else:
-                for h in range(2):
-                    offsets = lists[i][:, columns * h : columns * (h + 1)]
-                    nc.vector.tensor_copy(fetched[:, h * P : (h + 1) * P], y[:].indirect(offsets))
-                targets = [ps.tile([P, P], F32, name="bank_last%d" % h, tag="acc0" if h else "bank_last")[:] for h in range(2)]
-            for h in range(2):
-                nc.tensor.transpose(targets[h], fetched[:, h * P : (h + 1) * P], eye[:])
-                turned[i, h] = targets[h]
-        for i in range(TURNED):
-            for h in range(2):
+        for h in range(2):
+            for i in range(TURNED):
+                fetched = sb.tile([P, P], F32, name="fetched%d_%d" % (i, h))
+                offsets = lists[i][:, columns * h : columns * (h + 1)]
+                nc.scalar.activation(fetched[:], y[:].indirect(offsets), ACT.Copy)
+                last_unit = h == 1 and i == TURNED - 1
+                turned[i, h] = ps.tile([P, P], F32, name="bank%d_%d" % (i, h), tag="acc0" if last_unit else "bank%d_%d" % (i, h))[:]
+                nc.tensor.transpose(turned[i, h], fetched[:], eye[:])
+        for h in range(2):
+            for i in range(TURNED):
                 scaled = sb.tile([P, P], F32, name="scaled%d_%d" % (i, h))
                 factor = stay[:, h : h + 1] if i == 0 else coef[:, h, i - 1 : i]
                 nc.scalar.activation(scaled[:], turned[i, h], ACT.Copy, scale=factor)
                 nc.tensor.matmul(sums[h][:], scaled[:], eye[:], start=(i == 0), stop=(i == TURNED - 1), is_transpose=True)
 
-        term3 = sb.tile([P, V], F32, name="term3")
-        nc.vector.tensor_tensor(term3[:], y[:].indirect(lists[D - 1][:]), gate_full[D - 1][:], ALU.mult)
-        term4 = [sb.tile([P, P], F32, name="term4_%d" % h) for h in range(2)]
-        both = [sb.tile([P, P], F32, name="both%d" % h) for h in range(2)]
+        terms = {}
+        for i in range(TURNED, D):
+            terms[i] = sb.tile([P, V], F32, name="term%d" % i)
+            nc.vector.tensor_tensor(terms[i][:], y[:].indirect(lists[i][:]), gate_full[i][:], ALU.mult)
+        last = [sb.tile([P, P], F32, name="last%d" % h) for h in range(2)]
+        pair = sb.tile([P, V], F32, name="pair")
+        three = [sb.tile([P, P], F32, name="three%d" % h) for h in range(2)]
         for h in range(2):
             offsets = lists[D][:, columns * h : columns * (h + 1)]
-            nc.vector.tensor_tensor(term4[h][:], y[:].indirect(offsets), gate_full[D][:, h * P : (h + 1) * P], ALU.mult)
+            nc.vector.tensor_tensor(last[h][:], y[:].indirect(offsets), gate_full[D][:, h * P : (h + 1) * P], ALU.mult)
+            if h == 0:
+                nc.vector.tensor_tensor(pair[:], terms[D - 2][:], terms[D - 1][:], ALU.add)
         for h in range(2):
-            nc.vector.tensor_tensor(both[h][:], term3[:, h * P : (h + 1) * P], term4[h][:], ALU.add)
+            nc.vector.tensor_tensor(three[h][:], pair[:, h * P : (h + 1) * P], last[h][:], ALU.add)
         for h in range(2):
             res = sb.tile([P, P], F32, name="res%d" % h)
-            nc.vector.tensor_tensor(res[:], sums[h][:], both[h][:], ALU.add)
+            nc.vector.tensor_tensor(res[:], sums[h][:], three[h][:], ALU.add)
             nc.sync.dma_start(out=out[:, h * P : (h + 1) * P], in_=res[:])

@@ -18,48 +18,34 @@ ALU = mybir.AluOpType
 P = 128
 GROUP = 16
 PASSES = K // (4 * P)
-PLANES = 2 * PASSES
 HALF = S // 2
+SPLIT = HALF
+STEP = 128
 PIECES = ((0, 256), (256, 384), (384, 512))
 TURNED = 2
-CHUNKS = (
-    ((("scalar", 352), ("vector", 672)),),
-    ((("scalar", 352), ("vector", 672)),),
-    ((("scalar", 256), ("gpsimd", 256)), (("scalar", 128), ("vector", 384))),
-    ((("scalar", 384), ("gpsimd", 256)), (("scalar", 192), ("vector", 192))),
-)
 
 
 def tile_picked_grand_relu_e_kernel(tc, xT, w1, gate, offs, cen, pos1, pos2, pos3, pos4, out):
     nc = tc.nc
     with ExitStack() as ctx:
         sb = ctx.enter_context(tc.tile_pool(name="sb", bufs=1))
-        shared = ctx.enter_context(tc.tile_pool(name="shared", bufs=1))
         ps = ctx.enter_context(tc.psum_pool(name="ps", bufs=1))
 
-        x_rows = xT.rearrange("(g p u e) t -> g u p e t", p=P, u=2, e=2)
-        w_rows = w1.rearrange("(g p j) m -> g p j m", p=P, j=4)
+        x_rows = xT.rearrange("(g p j) t -> g j p t", p=P, j=4)
 
+        w_raw = sb.tile([P, PASSES, 4, N], F32, name="w_raw", align_bytes=64)
+        nc.sync.dma_start(out=w_raw[:], in_=w1.rearrange("(g p j) m -> p g j m", p=P, j=4))
         offs_sb = sb.tile([P, S // GROUP], U16, name="offs_sb")
+        nc.sync.dma_start(offs_sb[:], offs)
         gate_rows = sb.tile([P, V], F32, name="gate_rows")
         nc.gpsimd.memset(gate_rows[:], 0.0)
-        raw = {}
-        for q in range(PLANES):
-            b = 0
-            for c, shares in enumerate(CHUNKS[q]):
-                a, b = b, b + sum(n for engine, n in shares)
-                if b == T and q == PLANES - 1:
-                    raw[q, c] = shared.tile([P, 2, b - a], F32, name="raw_last", offset=0, align_bytes=64)
-                else:
-                    raw[q, c] = sb.tile([P, 2, b - a], F32, name="raw%d_%d" % (q, c), tag="raw%d_%d" % (q, c), align_bytes=64)
-                nc.sync.dma_start(out=raw[q, c][:], in_=x_rows[q // 2, q % 2, :, :, a:b])
-                if q == 0 and c == 0:
-                    nc.sync.dma_start(offs_sb[:], offs)
-                    nc.sync.dma_start(out=gate_rows[0:D, :], in_=gate[:, 0, :])
-        w_raw = []
+        rows = {}
         for g in range(PASSES):
-            w_raw.append(sb.tile([P, 4, N], F32, name="w_raw%d" % g, tag="w_raw%d" % g, align_bytes=64))
-            nc.sync.dma_start(out=w_raw[g][:], in_=w_rows[g])
+            for j in range(4):
+                rows[g, j] = sb.tile([P, T], F32, name="row%d_%d" % (g, j))
+                nc.sync.dma_start(out=rows[g, j][:], in_=x_rows[g, j])
+                if g == 0 and j == 0:
+                    nc.sync.dma_start(out=gate_rows[0:D, :], in_=gate[:, 0, :])
         lists = []
         for i, src in enumerate((cen, pos1, pos2, pos3, pos4)):
             lists.append(sb.tile([P, V // GROUP], U16, name="list%d" % i))
@@ -72,110 +58,86 @@ def tile_picked_grand_relu_e_kernel(tc, xT, w1, gate, offs, cen, pos1, pos2, pos
         eye = sb.tile([P, P], F32, name="eye")
         make_identity(nc, eye[:])
 
-        pairs = [sb.tile([P, T, 2], BF16, name="pairs%d" % q, align_bytes=64) for q in range(PLANES)]
-        both_planes = [sb.tile([P, 2, S], U32, name="words%d" % g) for g in range(PASSES)]
-        words = [both_planes[q // 2][:, q % 2, :] for q in range(PLANES)]
-        scales = [sb.tile([P, S], U8, name="scales%d" % g, align_bytes=64) for g in range(PASSES)]
-
-        def round_to_bf16(engine, dst, src):
-            if engine == "scalar":
-                nc.scalar.activation(dst, src, ACT.Copy)
-            elif engine == "vector":
-                nc.vector.tensor_copy(dst, src)
-            else:
-                nc.gpsimd.tensor_scalar(dst, src, 1.0, 0.0, ALU.mult, ALU.add)
-
-        def cast(q):
-            first = 0
-            for c, shares in enumerate(CHUNKS[q]):
-                src = raw[q, c][:].rearrange("p e t -> p t e")
-                a = 0
-                for engine, n in shares:
-                    round_to_bf16(engine, pairs[q][:, first + a : first + a + n, :], src[:, a : a + n, :])
-                    a += n
-                first += a
-
-        def gather(q, a, b):
-            window = pairs[q][:].rearrange("p t e -> p (t e)").bitcast(U32)
-            nc.vector.tensor_copy(words[q][:, a:b], window.indirect(offs_sb[:, a // GROUP : b // GROUP]))
-
-        def weave(groups, g, a, b):
-            woven = groups.rearrange("p n j -> p (n j)").bitcast(U32).rearrange("p (c i u) -> p c u i", i=4, u=2)
-            nc.scalar.copy(woven, both_planes[g][:, :, a:b].rearrange("p u (c i) -> p c u i", i=4))
-
         def quantise(packed, plane, groups):
             nc.vector.quantize_mx(out=packed.bitcast(FP8X4), scales=plane, in_=groups.rearrange("p n j -> p (n j)"))
+
+        w_bf = sb.tile([P, PASSES * N, 4], BF16, name="w_bf", align_bytes=64)
+        w_codes = sb.tile([P, PASSES * N], U32, name="w_codes", align_bytes=64)
+        w_scales = sb.tile([P, PASSES * N], U8, name="w_scales", align_bytes=64)
+        nc.vector.tensor_copy(w_bf[:, :N, :], w_raw[:, 0].rearrange("p j m -> p m j"))
+        nc.scalar.activation(w_bf[:, N:, :], w_raw[:, 1].rearrange("p j m -> p m j"), ACT.Copy)
+        quantise(w_codes[:], w_scales[:], w_bf[:])
 
         coef = sb.tile([P, 2, D], F32, name="coef")
         total = sb.tile([P, 2], F32, name="total")
         stay = sb.tile([P, 2], F32, name="stay")
-        gate_bank = ps.tile([P, 2, P], F32, name="gate_bank", tag="acc%d" % PIECES[-1][0])
+        gate_bank = ps.tile([P, 2, P], F32, name="gate_bank", tag="bank0_0")
         for h in range(2):
             nc.tensor.transpose(gate_bank[:, h, :], gate_rows[:, h * P : (h + 1) * P], eye[:])
         for h in range(2):
             nc.scalar.activation(coef[:, h, :], gate_bank[:, h, 0:D], ACT.Copy, accum_out=total[:, h : h + 1])
         nc.scalar.activation(stay[:], total[:], ACT.Copy, scale=-1.0, bias=1.0)
 
-        cast(0)
-        gather(0, 0, S)
-        cast(1)
-        for h in range(2):
-            gather(1, HALF * h, HALF * (h + 1))
-        cast(2)
-        picked0 = [sb.tile([P, HALF, 4], BF16, name="picked0_%d" % h, tag="raw2_%d" % h, align_bytes=64) for h in range(2)]
-        for h in range(2):
-            weave(picked0[h][:], 0, HALF * h, HALF * (h + 1))
-        codes0 = [sb.tile([P, HALF], U32, name="codes0_0", align_bytes=64)]
-        quantise(codes0[0][:], scales[0][:, :HALF], picked0[0][:])
-        gather(2, 0, S)
-        codes0.append(sb.tile([P, HALF], U32, name="codes0_1", align_bytes=64))
-        quantise(codes0[1][:], scales[0][:, HALF:], picked0[1][:])
-        cast(3)
-        codes1 = sb.tile([P, S], U32, name="codes1", align_bytes=64)
-        for a, b in PIECES:
-            gather(3, a, b)
-
-        w_bf = shared.tile([P, PASSES * N, 4], BF16, name="w_bf", offset=4 * HALF, align_bytes=64)
-        w_codes = sb.tile([P, PASSES * N], U32, name="w_codes", align_bytes=64)
-        w_scales = sb.tile([P, PASSES * N], U8, name="w_scales", align_bytes=64)
-        for g in range(PASSES):
-            round_to_bf16(
-                "gpsimd" if g else "scalar",
-                w_bf[:, g * N : (g + 1) * N, :],
-                w_raw[g][:].rearrange("p j m -> p m j"),
-            )
-        for g in range(PASSES):
-            cols = slice(g * N, (g + 1) * N)
-            quantise(w_codes[:, cols], w_scales[:, cols], w_bf[:, cols, :])
-        picked1 = sb.tile([P, S, 4], BF16, name="picked1", tag="w_raw0", align_bytes=64)
-        for a, b in PIECES:
-            weave(picked1[:, a:b, :], 1, a, b)
-
         y = sb.tile([P, S], F32, name="y")
-        acc = [ps.tile([P, b - a], F32, name="acc%d" % a, tag="acc%d" % a) for a, b in PIECES]
+        acc = [ps.tile([P, b - a], F32, name="acc%d" % i, tag="acc%d" % i) for i, (a, b) in enumerate(PIECES)]
 
-        def product(g, i):
+        def gather_stepped(groups, row, j, a, b):
+            nc.vector.tensor_copy(groups[:, a:b, j], row[:].indirect(offs_sb[:, a // GROUP : b // GROUP]))
+
+        def gather_plain(plain, row, j, a, b):
+            nc.scalar.activation(plain[:, j, a - SPLIT : b - SPLIT], row[:].indirect(offs_sb[:, a // GROUP : b // GROUP]), ACT.Copy)
+
+        def weave_on_gpsimd(dst, src):
+            nc.gpsimd.tensor_scalar(dst, src.rearrange("p j n -> p n j"), 1.0, 0.0, ALU.mult, ALU.add)
+
+        def product(g, i, codes, scales):
             a, b = PIECES[i]
-            codes = codes1[:, a:b] if g else codes0[a // HALF][:, a % HALF : a % HALF + b - a]
             nc.tensor.matmul_mx(
                 out=acc[i][:],
                 lhsT=w_codes[:, g * N : (g + 1) * N].bitcast(FP8X4),
                 lhsT_scale=w_scales[:, g * N : (g + 1) * N],
-                rhs=codes.bitcast(FP8X4),
-                rhs_scale=scales[g][:, a:b],
+                rhs=codes[:, a:b].bitcast(FP8X4),
+                rhs_scale=scales[:, a:b],
                 start=(g == 0),
                 stop=(g == PASSES - 1),
             )
 
+        codes = [sb.tile([P, S], U32, name="codes%d" % g, align_bytes=64) for g in range(PASSES)]
+        scales = [sb.tile([P, S], U8, name="scales%d" % g, align_bytes=64) for g in range(PASSES)]
+        plain = [sb.tile([P, 4, S - SPLIT], BF16, name="plain%d" % g, align_bytes=64) for g in range(PASSES)]
+
+        first = sb.tile([P, HALF, 4], BF16, name="first", tag="port", align_bytes=64)
+        for j in range(4):
+            gather_stepped(first, rows[0, j], j, 0, HALF)
+            gather_plain(plain[0], rows[0, j], j, HALF, S)
+        quantise(codes[0][:, :HALF], scales[0][:, :HALF], first[:])
+        second = sb.tile([P, HALF, 4], BF16, name="second", tag="port", align_bytes=64)
+        weave_on_gpsimd(second[:], plain[0][:])
+        quantise(codes[0][:, HALF:], scales[0][:, HALF:], second[:])
         for i in range(len(PIECES)):
-            product(0, i)
+            product(0, i, codes[0], scales[0])
+
+        stepped = sb.tile([P, HALF, 4], BF16, name="stepped", align_bytes=64)
+        woven = sb.tile([P, HALF, 4], BF16, name="woven", tag="port", align_bytes=64)
+        for j in range(3):
+            gather_stepped(stepped, rows[1, j], j, 0, HALF)
+            gather_plain(plain[1], rows[1, j], j, HALF, S)
+            if j == 1:
+                weave_on_gpsimd(woven[:, :, 0:2], plain[1][:, 0:2, :])
+        for a in (0, STEP):
+            gather_stepped(stepped, rows[1, 3], 3, a, a + STEP)
+            gather_plain(plain[1], rows[1, 3], 3, HALF + a, HALF + a + STEP)
+        for a in (0, STEP):
+            nc.scalar.copy(woven[:, a : a + STEP, 2:4], plain[1][:, 2:4, a : a + STEP].rearrange("p j n -> p n j"))
+        for a in range(0, S, STEP):
+            source = stepped[:, a : a + STEP, :] if a < HALF else woven[:, a - HALF : a - HALF + STEP, :]
+            quantise(codes[1][:, a : a + STEP], scales[1][:, a : a + STEP], source)
         for i, (a, b) in enumerate(PIECES):
-            quantise(codes1[:, a:b], scales[1][:, a:b], picked1[:, a:b, :])
-            product(1, i)
-            if i != 1:
-                nc.scalar.activation(y[:, a:b], acc[i][:], ACT.Relu)
-            else:
+            product(1, i, codes[1], scales[1])
+            if i == 1:
                 nc.vector.tensor_scalar_max(y[:, a:b], acc[i][:], 0.0)
+            else:
+                nc.scalar.activation(y[:, a:b], acc[i][:], ACT.Relu)
 
         sums = [ps.tile([P, P], F32, name="sums%d" % h) for h in range(2)]
         columns = P // GROUP
@@ -185,8 +147,7 @@ def tile_picked_grand_relu_e_kernel(tc, xT, w1, gate, offs, cen, pos1, pos2, pos
                 fetched = sb.tile([P, P], F32, name="fetched%d_%d" % (i, h))
                 offsets = lists[i][:, columns * h : columns * (h + 1)]
                 nc.scalar.activation(fetched[:], y[:].indirect(offsets), ACT.Copy)
-                last_unit = h == 1 and i == TURNED - 1
-                turned[i, h] = ps.tile([P, P], F32, name="bank%d_%d" % (i, h), tag="acc0" if last_unit else "bank%d_%d" % (i, h))[:]
+                turned[i, h] = ps.tile([P, P], F32, name="bank%d_%d" % (i, h), tag="acc%d" % i if h else "bank%d_0" % i)[:]
                 nc.tensor.transpose(turned[i, h], fetched[:], eye[:])
         for h in range(2):
             for i in range(TURNED):

@@ -18,8 +18,7 @@ ALU = mybir.AluOpType
 P = 128
 GROUP = 16
 PASSES = K // (4 * P)
-HALF = S // 2
-SPLIT = HALF
+SPLIT0 = 320
 STEP = 128
 PIECES = ((0, 256), (256, 384), (384, 512))
 TURNED = 2
@@ -31,21 +30,28 @@ def tile_picked_grand_relu_e_kernel(tc, xT, w1, gate, offs, cen, pos1, pos2, pos
         sb = ctx.enter_context(tc.tile_pool(name="sb", bufs=1))
         ps = ctx.enter_context(tc.psum_pool(name="ps", bufs=1))
 
-        x_rows = xT.rearrange("(g p j) t -> g j p t", p=P, j=4)
+        x_rows = xT.rearrange("(g p j) t -> g p j t", p=P, j=4)
+        w_rows = w1.rearrange("(g p j) m -> g p j m", p=P, j=4)
 
-        w_raw = sb.tile([P, PASSES, 4, N], F32, name="w_raw", align_bytes=64)
-        nc.sync.dma_start(out=w_raw[:], in_=w1.rearrange("(g p j) m -> p g j m", p=P, j=4))
         offs_sb = sb.tile([P, S // GROUP], U16, name="offs_sb")
-        nc.sync.dma_start(offs_sb[:], offs)
         gate_rows = sb.tile([P, V], F32, name="gate_rows")
-        nc.gpsimd.memset(gate_rows[:], 0.0)
+        nc.vector.memset(gate_rows[:, :P], 0.0)
+        nc.scalar.activation(gate_rows[:, P:], gate_rows[:, :P], ACT.Copy)
         rows = {}
+        for j in (0, 2):
+            two_rows = sb.tile([P, 2, T], F32, name="rows0_%d" % j)
+            nc.sync.dma_start(out=two_rows[:], in_=x_rows[0, :, j : j + 2, :])
+            rows[0, j], rows[0, j + 1] = two_rows[:, 0, :], two_rows[:, 1, :]
+            if j == 0:
+                nc.sync.dma_start(offs_sb[:], offs)
+        nc.sync.dma_start(out=gate_rows[0:D, :], in_=gate[:, 0, :])
+        for j in range(4):
+            rows[1, j] = sb.tile([P, T], F32, name="row1_%d" % j)[:]
+            nc.sync.dma_start(out=rows[1, j], in_=x_rows[1, :, j, :])
+        w_raw = []
         for g in range(PASSES):
-            for j in range(4):
-                rows[g, j] = sb.tile([P, T], F32, name="row%d_%d" % (g, j))
-                nc.sync.dma_start(out=rows[g, j][:], in_=x_rows[g, j])
-                if g == 0 and j == 0:
-                    nc.sync.dma_start(out=gate_rows[0:D, :], in_=gate[:, 0, :])
+            w_raw.append(sb.tile([P, 4, N], F32, name="w_raw%d" % g, align_bytes=64))
+            nc.sync.dma_start(out=w_raw[g][:], in_=w_rows[g])
         lists = []
         for i, src in enumerate((cen, pos1, pos2, pos3, pos4)):
             lists.append(sb.tile([P, V // GROUP], U16, name="list%d" % i))
@@ -61,13 +67,6 @@ def tile_picked_grand_relu_e_kernel(tc, xT, w1, gate, offs, cen, pos1, pos2, pos
         def quantise(packed, plane, groups):
             nc.vector.quantize_mx(out=packed.bitcast(FP8X4), scales=plane, in_=groups.rearrange("p n j -> p (n j)"))
 
-        w_bf = sb.tile([P, PASSES * N, 4], BF16, name="w_bf", align_bytes=64)
-        w_codes = sb.tile([P, PASSES * N], U32, name="w_codes", align_bytes=64)
-        w_scales = sb.tile([P, PASSES * N], U8, name="w_scales", align_bytes=64)
-        nc.vector.tensor_copy(w_bf[:, :N, :], w_raw[:, 0].rearrange("p j m -> p m j"))
-        nc.scalar.activation(w_bf[:, N:, :], w_raw[:, 1].rearrange("p j m -> p m j"), ACT.Copy)
-        quantise(w_codes[:], w_scales[:], w_bf[:])
-
         coef = sb.tile([P, 2, D], F32, name="coef")
         total = sb.tile([P, 2], F32, name="total")
         stay = sb.tile([P, 2], F32, name="stay")
@@ -80,60 +79,67 @@ def tile_picked_grand_relu_e_kernel(tc, xT, w1, gate, offs, cen, pos1, pos2, pos
 
         y = sb.tile([P, S], F32, name="y")
         acc = [ps.tile([P, b - a], F32, name="acc%d" % i, tag="acc%d" % i) for i, (a, b) in enumerate(PIECES)]
+        codes = [sb.tile([P, S], U32, name="codes%d" % g, align_bytes=64) for g in range(PASSES)]
+        scales = [sb.tile([P, S], U8, name="scales%d" % g, align_bytes=64) for g in range(PASSES)]
+        w_codes = sb.tile([P, PASSES * N], U32, name="w_codes", align_bytes=64)
+        w_scales = sb.tile([P, PASSES * N], U8, name="w_scales", align_bytes=64)
 
-        def gather_stepped(groups, row, j, a, b):
-            nc.vector.tensor_copy(groups[:, a:b, j], row[:].indirect(offs_sb[:, a // GROUP : b // GROUP]))
+        def picked(row, a, b):
+            return row.indirect(offs_sb[:, a // GROUP : b // GROUP])
 
-        def gather_plain(plain, row, j, a, b):
-            nc.scalar.activation(plain[:, j, a - SPLIT : b - SPLIT], row[:].indirect(offs_sb[:, a // GROUP : b // GROUP]), ACT.Copy)
+        def side_by_side(plain):
+            return plain.rearrange("p j n -> p n j")
 
-        def weave_on_gpsimd(dst, src):
-            nc.gpsimd.tensor_scalar(dst, src.rearrange("p j n -> p n j"), 1.0, 0.0, ALU.mult, ALU.add)
-
-        def product(g, i, codes, scales):
+        def product(g, i):
             a, b = PIECES[i]
             nc.tensor.matmul_mx(
                 out=acc[i][:],
                 lhsT=w_codes[:, g * N : (g + 1) * N].bitcast(FP8X4),
                 lhsT_scale=w_scales[:, g * N : (g + 1) * N],
-                rhs=codes[:, a:b].bitcast(FP8X4),
-                rhs_scale=scales[:, a:b],
+                rhs=codes[g][:, a:b].bitcast(FP8X4),
+                rhs_scale=scales[g][:, a:b],
                 start=(g == 0),
                 stop=(g == PASSES - 1),
             )
 
-        codes = [sb.tile([P, S], U32, name="codes%d" % g, align_bytes=64) for g in range(PASSES)]
-        scales = [sb.tile([P, S], U8, name="scales%d" % g, align_bytes=64) for g in range(PASSES)]
-        plain = [sb.tile([P, 4, S - SPLIT], BF16, name="plain%d" % g, align_bytes=64) for g in range(PASSES)]
-
-        first = sb.tile([P, HALF, 4], BF16, name="first", tag="port", align_bytes=64)
+        groups0 = sb.tile([P, S, 4], BF16, name="groups0", tag="port", align_bytes=64)
+        plain0 = sb.tile([P, 4, S - SPLIT0], F32, name="plain0")
         for j in range(4):
-            gather_stepped(first, rows[0, j], j, 0, HALF)
-            gather_plain(plain[0], rows[0, j], j, HALF, S)
-        quantise(codes[0][:, :HALF], scales[0][:, :HALF], first[:])
-        second = sb.tile([P, HALF, 4], BF16, name="second", tag="port", align_bytes=64)
-        weave_on_gpsimd(second[:], plain[0][:])
-        quantise(codes[0][:, HALF:], scales[0][:, HALF:], second[:])
-        for i in range(len(PIECES)):
-            product(0, i, codes[0], scales[0])
+            nc.scalar.activation(plain0[:, j, :], picked(rows[0, j], SPLIT0, S), ACT.Copy)
+            nc.vector.tensor_copy(groups0[:, :SPLIT0, j], picked(rows[0, j], 0, SPLIT0))
+        nc.scalar.activation(groups0[:, SPLIT0:, :], side_by_side(plain0[:]), ACT.Copy)
+        quantise(codes[0][:], scales[0][:], groups0[:])
 
-        stepped = sb.tile([P, HALF, 4], BF16, name="stepped", align_bytes=64)
-        woven = sb.tile([P, HALF, 4], BF16, name="woven", tag="port", align_bytes=64)
+        stepped = sb.tile([P, STEP, 4], BF16, name="stepped", align_bytes=64)
+        plain1 = sb.tile([P, 4, S - STEP], BF16, name="plain1")
+        woven = sb.tile([P, S - STEP, 4], BF16, name="woven", tag="port", align_bytes=64)
         for j in range(3):
-            gather_stepped(stepped, rows[1, j], j, 0, HALF)
-            gather_plain(plain[1], rows[1, j], j, HALF, S)
+            nc.vector.tensor_copy(stepped[:, :, j], picked(rows[1, j], 0, STEP))
+            nc.scalar.activation(plain1[:, j, :], picked(rows[1, j], STEP, S), ACT.Copy)
             if j == 1:
-                weave_on_gpsimd(woven[:, :, 0:2], plain[1][:, 0:2, :])
-        for a in (0, STEP):
-            gather_stepped(stepped, rows[1, 3], 3, a, a + STEP)
-            gather_plain(plain[1], rows[1, 3], 3, HALF + a, HALF + a + STEP)
-        for a in (0, STEP):
-            nc.scalar.copy(woven[:, a : a + STEP, 2:4], plain[1][:, 2:4, a : a + STEP].rearrange("p j n -> p n j"))
-        for a in range(0, S, STEP):
-            source = stepped[:, a : a + STEP, :] if a < HALF else woven[:, a - HALF : a - HALF + STEP, :]
+                nc.gpsimd.tensor_scalar(woven[:, :, 0:2], side_by_side(plain1[:, 0:2, :]), 1.0, 0.0, ALU.mult, ALU.add)
+        nc.vector.tensor_copy(stepped[:, :, 3], picked(rows[1, 3], 0, STEP))
+        for a in range(0, S - STEP, STEP):
+            nc.scalar.activation(plain1[:, 3, a : a + STEP], picked(rows[1, 3], STEP + a, 2 * STEP + a), ACT.Copy)
+        for a in range(0, S - STEP, STEP):
+            nc.scalar.copy(woven[:, a : a + STEP, 2:4], side_by_side(plain1[:, 2:4, a : a + STEP]))
+
+        def quantise_nodes(a):
+            source = woven[:, a - STEP : a, :] if a else stepped[:]
             quantise(codes[1][:, a : a + STEP], scales[1][:, a : a + STEP], source)
+
+        w_bf = [sb.tile([P, N, 4], BF16, name="w_bf%d" % g, align_bytes=64) for g in range(PASSES)]
+        for g in range(PASSES):
+            cols = slice(g * N, (g + 1) * N)
+            nc.vector.tensor_copy(w_bf[g][:], w_raw[g][:].rearrange("p j m -> p m j"))
+            quantise_nodes(g * STEP)
+            quantise(w_codes[:, cols], w_scales[:, cols], w_bf[g][:])
+        for i in range(len(PIECES)):
+            product(0, i)
+        for a in range(PASSES * STEP, S, STEP):
+            quantise_nodes(a)
         for i, (a, b) in enumerate(PIECES):
-            product(1, i, codes[1], scales[1])
+            product(1, i)
             if i == 1:
                 nc.vector.tensor_scalar_max(y[:, a:b], acc[i][:], 0.0)
             else:

@@ -20,7 +20,7 @@ GROUP = 16
 PASSES = K // (4 * P)
 SPLIT0 = 320
 STEP = 128
-PIECES = ((0, 256), (256, 384), (384, 512))
+PIECES = ((0, 128), (128, 384), (384, 512))
 TURNED = 2
 
 
@@ -44,7 +44,7 @@ def tile_picked_grand_relu_e_kernel(tc, xT, w1, gate, offs, cen, pos1, pos2, pos
             rows[0, j], rows[0, j + 1] = two_rows[:, 0, :], two_rows[:, 1, :]
             if j == 0:
                 nc.sync.dma_start(offs_sb[:], offs)
-        nc.sync.dma_start(out=gate_rows[0:D, :], in_=gate[:, 0, :])
+                nc.sync.dma_start(out=gate_rows[0:D, :], in_=gate[:, 0, :])
         for j in range(4):
             rows[1, j] = sb.tile([P, T], F32, name="row1_%d" % j)[:]
             nc.sync.dma_start(out=rows[1, j], in_=x_rows[1, :, j, :])
@@ -79,7 +79,8 @@ def tile_picked_grand_relu_e_kernel(tc, xT, w1, gate, offs, cen, pos1, pos2, pos
 
         y = sb.tile([P, S], F32, name="y")
         acc = [ps.tile([P, b - a], F32, name="acc%d" % i, tag="acc%d" % i) for i, (a, b) in enumerate(PIECES)]
-        codes = [sb.tile([P, S], U32, name="codes%d" % g, align_bytes=64) for g in range(PASSES)]
+        codes0 = sb.tile([P, S], U32, name="codes0", align_bytes=64)
+        codes1 = {}
         scales = [sb.tile([P, S], U8, name="scales%d" % g, align_bytes=64) for g in range(PASSES)]
         w_codes = sb.tile([P, PASSES * N], U32, name="w_codes", align_bytes=64)
         w_scales = sb.tile([P, PASSES * N], U8, name="w_scales", align_bytes=64)
@@ -96,7 +97,7 @@ def tile_picked_grand_relu_e_kernel(tc, xT, w1, gate, offs, cen, pos1, pos2, pos
                 out=acc[i][:],
                 lhsT=w_codes[:, g * N : (g + 1) * N].bitcast(FP8X4),
                 lhsT_scale=w_scales[:, g * N : (g + 1) * N],
-                rhs=codes[g][:, a:b].bitcast(FP8X4),
+                rhs=(codes1[i][:] if g else codes0[:, a:b]).bitcast(FP8X4),
                 rhs_scale=scales[g][:, a:b],
                 start=(g == 0),
                 stop=(g == PASSES - 1),
@@ -107,8 +108,8 @@ def tile_picked_grand_relu_e_kernel(tc, xT, w1, gate, offs, cen, pos1, pos2, pos
         for j in range(4):
             nc.scalar.activation(plain0[:, j, :], picked(rows[0, j], SPLIT0, S), ACT.Copy)
             nc.vector.tensor_copy(groups0[:, :SPLIT0, j], picked(rows[0, j], 0, SPLIT0))
-        nc.scalar.activation(groups0[:, SPLIT0:, :], side_by_side(plain0[:]), ACT.Copy)
-        quantise(codes[0][:], scales[0][:], groups0[:])
+        nc.gpsimd.tensor_scalar(groups0[:, SPLIT0:, :], side_by_side(plain0[:]), 1.0, 0.0, ALU.mult, ALU.add)
+        quantise(codes0[:], scales[0][:], groups0[:])
 
         stepped = sb.tile([P, STEP, 4], BF16, name="stepped", align_bytes=64)
         plain1 = sb.tile([P, 4, S - STEP], BF16, name="plain1")
@@ -125,15 +126,19 @@ def tile_picked_grand_relu_e_kernel(tc, xT, w1, gate, offs, cen, pos1, pos2, pos
             nc.scalar.copy(woven[:, a : a + STEP, 2:4], side_by_side(plain1[:, 2:4, a : a + STEP]))
 
         def quantise_nodes(a):
+            i = max(n for n, (first, end) in enumerate(PIECES) if first <= a)
+            first, end = PIECES[i]
+            if a == first:
+                codes1[i] = sb.tile([P, end - first], U32, name="codes1_%d" % i, tag="w_bf0" if i == 1 else "codes1_%d" % i, align_bytes=64)
             source = woven[:, a - STEP : a, :] if a else stepped[:]
-            quantise(codes[1][:, a : a + STEP], scales[1][:, a : a + STEP], source)
+            quantise(codes1[i][:, a - first : a - first + STEP], scales[1][:, a : a + STEP], source)
 
-        w_bf = [sb.tile([P, N, 4], BF16, name="w_bf%d" % g, align_bytes=64) for g in range(PASSES)]
         for g in range(PASSES):
             cols = slice(g * N, (g + 1) * N)
-            nc.vector.tensor_copy(w_bf[g][:], w_raw[g][:].rearrange("p j m -> p m j"))
+            w_bf = sb.tile([P, N, 4], BF16, name="w_bf%d" % g, tag="w_bf%d" % g, align_bytes=64)
+            nc.vector.tensor_copy(w_bf[:], w_raw[g][:].rearrange("p j m -> p m j"))
             quantise_nodes(g * STEP)
-            quantise(w_codes[:, cols], w_scales[:, cols], w_bf[g][:])
+            quantise(w_codes[:, cols], w_scales[:, cols], w_bf[:])
         for i in range(len(PIECES)):
             product(0, i)
         for a in range(PASSES * STEP, S, STEP):

@@ -35,8 +35,7 @@ def tile_picked_grand_relu_e_kernel(tc, xT, w1, gate, offs, cen, pos1, pos2, pos
 
         offs_sb = sb.tile([P, S // GROUP], U16, name="offs_sb")
         gate_rows = sb.tile([P, V], F32, name="gate_rows")
-        nc.vector.memset(gate_rows[:, :P], 0.0)
-        nc.scalar.activation(gate_rows[:, P:], gate_rows[:, :P], ACT.Copy)
+        nc.gpsimd.memset(gate_rows[:], 0.0)
         rows = {}
         for j in (0, 2):
             two_rows = sb.tile([P, 2, T], F32, name="rows0_%d" % j)
@@ -62,7 +61,9 @@ def tile_picked_grand_relu_e_kernel(tc, xT, w1, gate, offs, cen, pos1, pos2, pos
             nc.sync.dma_start(out=gate_full[i][:], in_=gate[i - 1])
 
         eye = sb.tile([P, P], F32, name="eye")
-        make_identity(nc, eye[:])
+        nc.vector.memset(eye[:, : P // 2], 0.0)
+        nc.scalar.activation(eye[:, P // 2 :], eye[:, : P // 2], ACT.Copy)
+        make_identity(nc, eye[:], nomemset=True)
 
         def quantise(packed, plane, groups):
             nc.vector.quantize_mx(out=packed.bitcast(FP8X4), scales=plane, in_=groups.rearrange("p n j -> p (n j)"))

@@ -18,7 +18,7 @@ ALU = mybir.AluOpType
 P = 128
 GROUP = 16
 PASSES = K // (4 * P)
-SPLIT0 = 320
+SPLIT0 = 256
 STEP = 128
 PIECES = ((0, 128), (128, 384), (384, 512))
 TURNED = 2
@@ -109,7 +109,9 @@ def tile_picked_grand_relu_e_kernel(tc, xT, w1, gate, offs, cen, pos1, pos2, pos
         for j in range(4):
             nc.scalar.activation(plain0[:, j, :], picked(rows[0, j], SPLIT0, S), ACT.Copy)
             nc.vector.tensor_copy(groups0[:, :SPLIT0, j], picked(rows[0, j], 0, SPLIT0))
-        nc.gpsimd.tensor_scalar(groups0[:, SPLIT0:, :], side_by_side(plain0[:]), 1.0, 0.0, ALU.mult, ALU.add)
+            if j % 2:
+                pair = slice(j - 1, j + 1)
+                nc.gpsimd.tensor_scalar(groups0[:, SPLIT0:, pair], side_by_side(plain0[:, pair, :]), 1.0, 0.0, ALU.mult, ALU.add)
         quantise(codes0[:], scales[0][:], groups0[:])
 
         stepped = sb.tile([P, STEP, 4], BF16, name="stepped", align_bytes=64)

@@ -21,7 +21,7 @@ PASSES = K // (4 * P)
 SPLIT0 = 256
 STEP = 128
 PIECES = ((0, 128), (128, 384), (384, 512))
-TURNED = 2
+TURNED = ((0, 0), (2, 0), (1, 0), (2, 1), (1, 1), (0, 1))
 
 
 def tile_picked_grand_relu_e_kernel(tc, xT, w1, gate, offs, cen, pos1, pos2, pos3, pos4, out):
@@ -56,7 +56,7 @@ def tile_picked_grand_relu_e_kernel(tc, xT, w1, gate, offs, cen, pos1, pos2, pos
             lists.append(sb.tile([P, V // GROUP], U16, name="list%d" % i))
             nc.sync.dma_start(lists[i][:], src)
         gate_full = {}
-        for i in range(TURNED, D + 1):
+        for i in (3, 4):
             gate_full[i] = sb.tile([P, V], F32, name="gate_full%d" % i)
             nc.sync.dma_start(out=gate_full[i][:], in_=gate[i - 1])
 
@@ -71,7 +71,7 @@ def tile_picked_grand_relu_e_kernel(tc, xT, w1, gate, offs, cen, pos1, pos2, pos
         coef = sb.tile([P, 2, D], F32, name="coef")
         total = sb.tile([P, 2], F32, name="total")
         stay = sb.tile([P, 2], F32, name="stay")
-        gate_bank = ps.tile([P, 2, P], F32, name="gate_bank", tag="bank0_0")
+        gate_bank = ps.tile([P, 2, P], F32, name="gate_bank", tag="bank0")
         for h in range(2):
             nc.tensor.transpose(gate_bank[:, h, :], gate_rows[:, h * P : (h + 1) * P], eye[:])
         for h in range(2):
@@ -154,37 +154,36 @@ def tile_picked_grand_relu_e_kernel(tc, xT, w1, gate, offs, cen, pos1, pos2, pos
                 nc.scalar.activation(y[:, a:b], acc[i][:], ACT.Relu)
 
         sums = [ps.tile([P, P], F32, name="sums%d" % h) for h in range(2)]
-        columns = P // GROUP
-        turned = {}
-        for h in range(2):
-            for i in range(TURNED):
-                fetched = sb.tile([P, P], F32, name="fetched%d_%d" % (i, h))
-                offsets = lists[i][:, columns * h : columns * (h + 1)]
-                nc.scalar.activation(fetched[:], y[:].indirect(offsets), ACT.Copy)
-                turned[i, h] = ps.tile([P, P], F32, name="bank%d_%d" % (i, h), tag="acc%d" % i if h else "bank%d_0" % i)[:]
-                nc.tensor.transpose(turned[i, h], fetched[:], eye[:])
-        for h in range(2):
-            for i in range(TURNED):
-                scaled = sb.tile([P, P], F32, name="scaled%d_%d" % (i, h))
-                factor = stay[:, h : h + 1] if i == 0 else coef[:, h, i - 1 : i]
-                nc.scalar.activation(scaled[:], turned[i, h], ACT.Copy, scale=factor)
-                nc.tensor.matmul(sums[h][:], scaled[:], eye[:], start=(i == 0), stop=(i == TURNED - 1), is_transpose=True)
 
-        terms = {}
-        for i in range(TURNED, D):
-            terms[i] = sb.tile([P, V], F32, name="term%d" % i)
-            nc.vector.tensor_tensor(terms[i][:], y[:].indirect(lists[i][:]), gate_full[i][:], ALU.mult)
-        last = [sb.tile([P, P], F32, name="last%d" % h) for h in range(2)]
-        pair = sb.tile([P, V], F32, name="pair")
-        three = [sb.tile([P, P], F32, name="three%d" % h) for h in range(2)]
+        def looked_up(i, a, b):
+            return y[:].indirect(lists[i][:, a // GROUP : b // GROUP])
+
+        fetched = [sb.tile([P, V], F32, name="fetched%d" % i) for i in range(3)]
+        nc.vector.tensor_copy(fetched[2][:], looked_up(2, 0, V))
+        nc.vector.tensor_copy(fetched[1][:, P:], looked_up(1, P, V))
+        for i, h in ((0, 0), (1, 0), (0, 1)):
+            nc.scalar.activation(fetched[i][:, h * P : (h + 1) * P], looked_up(i, h * P, (h + 1) * P), ACT.Copy)
+        turned = {}
+        for n, (i, h) in enumerate(TURNED):
+            turned[i, h] = ps.tile([P, P], F32, name="bank%d_%d" % (i, h), tag="bank%d" % n if n < 3 else "acc%d" % (n - 3))[:]
+            nc.tensor.transpose(turned[i, h], fetched[i][:, h * P : (h + 1) * P], eye[:])
+        for n, (i, h) in enumerate(TURNED):
+            scaled = sb.tile([P, P], F32, name="scaled%d_%d" % (i, h))
+            factor = stay[:, h : h + 1] if i == 0 else coef[:, h, i - 1 : i]
+            nc.scalar.activation(scaled[:], turned[i, h], ACT.Copy, scale=factor)
+            opens = n == 0 or TURNED[n - 1][1] != h
+            closes = n == len(TURNED) - 1 or TURNED[n + 1][1] != h
+            nc.tensor.matmul(sums[h][:], scaled[:], eye[:], start=opens, stop=closes, is_transpose=True)
+
+        term3 = sb.tile([P, V], F32, name="term3")
+        nc.vector.tensor_tensor(term3[:], looked_up(3, 0, V), gate_full[3][:], ALU.mult)
+        term4 = [sb.tile([P, P], F32, name="term4_%d" % h) for h in range(2)]
+        fused = [sb.tile([P, P], F32, name="fused%d" % h) for h in range(2)]
         for h in range(2):
-            offsets = lists[D][:, columns * h : columns * (h + 1)]
-            nc.vector.tensor_tensor(last[h][:], y[:].indirect(offsets), gate_full[D][:, h * P : (h + 1) * P], ALU.mult)
-            if h == 0:
-                nc.vector.tensor_tensor(pair[:], terms[D - 2][:], terms[D - 1][:], ALU.add)
+            nc.vector.tensor_tensor(term4[h][:], looked_up(4, h * P, (h + 1) * P), gate_full[4][:, h * P : (h + 1) * P], ALU.mult)
         for h in range(2):
-            nc.vector.tensor_tensor(three[h][:], pair[:, h * P : (h + 1) * P], last[h][:], ALU.add)
+            nc.vector.tensor_tensor(fused[h][:], term3[:, h * P : (h + 1) * P], term4[h][:], ALU.add)
         for h in range(2):
             res = sb.tile([P, P], F32, name="res%d" % h)
-            nc.vector.tensor_tensor(res[:], sums[h][:], three[h][:], ALU.add)
+            nc.vector.tensor_tensor(res[:], sums[h][:], fused[h][:], ALU.add)
             nc.sync.dma_start(out=out[:, h * P : (h + 1) * P], in_=res[:])

@@ -19,6 +19,7 @@ P = 128
 GROUP = 16
 PASSES = K // (4 * P)
 SPLIT0 = 256
+SPARE = 64
 STEP = 128
 PIECES = ((0, 128), (128, 384), (384, 512))
 TURNED = ((0, 0), (2, 0), (1, 0), (2, 1), (1, 1), (0, 1))
@@ -123,8 +124,9 @@ def tile_picked_grand_relu_e_kernel(tc, xT, w1, gate, offs, cen, pos1, pos2, pos
             if j == 1:
                 nc.gpsimd.tensor_scalar(woven[:, :, 0:2], side_by_side(plain1[:, 0:2, :]), 1.0, 0.0, ALU.mult, ALU.add)
         nc.vector.tensor_copy(stepped[:, :, 3], picked(rows[1, 3], 0, STEP))
-        for a in range(0, S - STEP, STEP):
-            nc.scalar.activation(plain1[:, 3, a : a + STEP], picked(rows[1, 3], STEP + a, 2 * STEP + a), ACT.Copy)
+        nc.vector.tensor_copy(plain1[:, 3, S - STEP - SPARE :], picked(rows[1, 3], S - SPARE, S))
+        for a, b in ((STEP, 2 * STEP), (2 * STEP, S - SPARE)):
+            nc.scalar.activation(plain1[:, 3, a - STEP : b - STEP], picked(rows[1, 3], a, b), ACT.Copy)
         for a in range(0, S - STEP, STEP):
             nc.scalar.copy(woven[:, a : a + STEP, 2:4], side_by_side(plain1[:, 2:4, a : a + STEP]))
 
@@ -139,7 +141,7 @@ def tile_picked_grand_relu_e_kernel(tc, xT, w1, gate, offs, cen, pos1, pos2, pos
         for g in range(PASSES):
             cols = slice(g * N, (g + 1) * N)
             w_bf = sb.tile([P, N, 4], BF16, name="w_bf%d" % g, tag="w_bf%d" % g, align_bytes=64)
-            nc.vector.tensor_copy(w_bf[:], w_raw[g][:].rearrange("p j m -> p m j"))
+            nc.vector.tensor_copy(w_bf[:].rearrange("p (c i) j -> p c j i", i=4), w_raw[g][:].rearrange("p j (c i) -> p c j i", i=4))
             quantise_nodes(g * STEP)
             quantise(w_codes[:, cols], w_scales[:, cols], w_bf[:])
         for i in range(len(PIECES)):

@@ -21,8 +21,8 @@ PASSES = K // (4 * P)
 SPLIT0 = 256
 SPARE = 64
 STEP = 128
-PIECES = ((0, 128), (128, 384), (384, 512))
-TURNED = ((0, 0), (2, 0), (1, 0), (2, 1), (1, 1), (0, 1))
+PIECES = ((0, 128), (128, 256), (256, 384), (384, 512))
+TURNED = ((1, 1), (0, 0), (0, 1), (2, 1), (2, 0), (1, 0))
 
 
 def tile_picked_grand_relu_e_kernel(tc, xT, w1, gate, offs, cen, pos1, pos2, pos3, pos4, out):
@@ -150,7 +150,7 @@ def tile_picked_grand_relu_e_kernel(tc, xT, w1, gate, offs, cen, pos1, pos2, pos
             quantise_nodes(a)
         for i, (a, b) in enumerate(PIECES):
             product(1, i)
-            if i == 1:
+            if i == 2:
                 nc.vector.tensor_scalar_max(y[:, a:b], acc[i][:], 0.0)
             else:
                 nc.scalar.activation(y[:, a:b], acc[i][:], ACT.Relu)
@@ -161,31 +161,31 @@ def tile_picked_grand_relu_e_kernel(tc, xT, w1, gate, offs, cen, pos1, pos2, pos
             return y[:].indirect(lists[i][:, a // GROUP : b // GROUP])
 
         fetched = [sb.tile([P, V], F32, name="fetched%d" % i) for i in range(3)]
-        nc.vector.tensor_copy(fetched[2][:], looked_up(2, 0, V))
         nc.vector.tensor_copy(fetched[1][:, P:], looked_up(1, P, V))
-        for i, h in ((0, 0), (1, 0), (0, 1)):
+        nc.vector.tensor_copy(fetched[2][:], looked_up(2, 0, V))
+        for i, h in ((0, 0), (0, 1), (1, 0)):
             nc.scalar.activation(fetched[i][:, h * P : (h + 1) * P], looked_up(i, h * P, (h + 1) * P), ACT.Copy)
         turned = {}
         for n, (i, h) in enumerate(TURNED):
-            turned[i, h] = ps.tile([P, P], F32, name="bank%d_%d" % (i, h), tag="bank%d" % n if n < 3 else "acc%d" % (n - 3))[:]
+            turned[i, h] = ps.tile([P, P], F32, name="bank%d_%d" % (i, h), tag="bank%d" % n if n < 2 else "acc%d" % (n - 2))[:]
             nc.tensor.transpose(turned[i, h], fetched[i][:, h * P : (h + 1) * P], eye[:])
         for n, (i, h) in enumerate(TURNED):
             scaled = sb.tile([P, P], F32, name="scaled%d_%d" % (i, h))
             factor = stay[:, h : h + 1] if i == 0 else coef[:, h, i - 1 : i]
             nc.scalar.activation(scaled[:], turned[i, h], ACT.Copy, scale=factor)
-            opens = n == 0 or TURNED[n - 1][1] != h
-            closes = n == len(TURNED) - 1 or TURNED[n + 1][1] != h
+            opens = all(other != h for term, other in TURNED[:n])
+            closes = all(other != h for term, other in TURNED[n + 1 :])
             nc.tensor.matmul(sums[h][:], scaled[:], eye[:], start=opens, stop=closes, is_transpose=True)
 
         term3 = sb.tile([P, V], F32, name="term3")
         nc.vector.tensor_tensor(term3[:], looked_up(3, 0, V), gate_full[3][:], ALU.mult)
         term4 = [sb.tile([P, P], F32, name="term4_%d" % h) for h in range(2)]
         fused = [sb.tile([P, P], F32, name="fused%d" % h) for h in range(2)]
-        for h in range(2):
+        for h in (1, 0):
             nc.vector.tensor_tensor(term4[h][:], looked_up(4, h * P, (h + 1) * P), gate_full[4][:, h * P : (h + 1) * P], ALU.mult)
-        for h in range(2):
+        for h in (1, 0):
             nc.vector.tensor_tensor(fused[h][:], term3[:, h * P : (h + 1) * P], term4[h][:], ALU.add)
-        for h in range(2):
+        for h in (1, 0):
             res = sb.tile([P, P], F32, name="res%d" % h)
             nc.vector.tensor_tensor(res[:], sums[h][:], fused[h][:], ALU.add)
             nc.sync.dma_start(out=out[:, h * P : (h + 1) * P], in_=res[:])

@@ -30,6 +30,7 @@ def tile_picked_grand_relu_e_kernel(tc, xT, w1, gate, offs, cen, pos1, pos2, pos
     with ExitStack() as ctx:
         sb = ctx.enter_context(tc.tile_pool(name="sb", bufs=1))
         ps = ctx.enter_context(tc.psum_pool(name="ps", bufs=1))
+        shared = ctx.enter_context(tc.tile_pool(name="shared", bufs=1))
 
         x_rows = xT.rearrange("(g p j) t -> g p j t", p=P, j=4)
         w_rows = w1.rearrange("(g p j) m -> g p j m", p=P, j=4)
@@ -83,9 +84,8 @@ def tile_picked_grand_relu_e_kernel(tc, xT, w1, gate, offs, cen, pos1, pos2, pos
         acc = [ps.tile([P, b - a], F32, name="acc%d" % i, tag="acc%d" % i) for i, (a, b) in enumerate(PIECES)]
         codes0 = sb.tile([P, S], U32, name="codes0", align_bytes=64)
         codes1 = {}
-        scales = [sb.tile([P, S], U8, name="scales%d" % g, align_bytes=64) for g in range(PASSES)]
-        w_codes = sb.tile([P, PASSES * N], U32, name="w_codes", align_bytes=64)
-        w_scales = sb.tile([P, PASSES * N], U8, name="w_scales", align_bytes=64)
+        scales0 = sb.tile([P, S], U8, name="scales0", align_bytes=64)
+        w_codes, w_scales, scales1 = {}, {}, {}
 
         def picked(row, a, b):
             return row.indirect(offs_sb[:, a // GROUP : b // GROUP])
@@ -97,15 +97,15 @@ def tile_picked_grand_relu_e_kernel(tc, xT, w1, gate, offs, cen, pos1, pos2, pos
             a, b = PIECES[i]
             nc.tensor.matmul_mx(
                 out=acc[i][:],
-                lhsT=w_codes[:, g * N : (g + 1) * N].bitcast(FP8X4),
-                lhsT_scale=w_scales[:, g * N : (g + 1) * N],
-                rhs=(codes1[i][:] if g else codes0[:, a:b]).bitcast(FP8X4),
-                rhs_scale=scales[g][:, a:b],
+                lhsT=w_codes[g].bitcast(FP8X4),
+                lhsT_scale=w_scales[g],
+                rhs=(codes1[i] if g else codes0[:, a:b]).bitcast(FP8X4),
+                rhs_scale=scales1[i] if g else scales0[:, a:b],
                 start=(g == 0),
                 stop=(g == PASSES - 1),
             )
 
-        groups0 = sb.tile([P, S, 4], BF16, name="groups0", tag="port", align_bytes=64)
+        groups0 = shared.tile([P, S, 4], BF16, name="groups0", offset=0, align_bytes=64)
         plain0 = sb.tile([P, 4, S - SPLIT0], F32, name="plain0")
         for j in range(4):
             nc.scalar.activation(plain0[:, j, :], picked(rows[0, j], SPLIT0, S), ACT.Copy)
@@ -113,41 +113,54 @@ def tile_picked_grand_relu_e_kernel(tc, xT, w1, gate, offs, cen, pos1, pos2, pos
             if j % 2:
                 pair = slice(j - 1, j + 1)
                 nc.gpsimd.tensor_scalar(groups0[:, SPLIT0:, pair], side_by_side(plain0[:, pair, :]), 1.0, 0.0, ALU.mult, ALU.add)
-        quantise(codes0[:], scales[0][:], groups0[:])
+        quantise(codes0[:], scales0[:], groups0[:])
 
-        stepped = sb.tile([P, STEP, 4], BF16, name="stepped", align_bytes=64)
+        joint = sb.tile([P, STEP + N, 4], BF16, name="joint", tag="joint", align_bytes=64)
+        joint_codes = sb.tile([P, STEP + N], U32, name="joint_codes", align_bytes=64)
+        joint_scales = sb.tile([P, STEP + N], U8, name="joint_scales", align_bytes=64)
+        stepped = joint[:, :STEP, :]
         plain1 = sb.tile([P, 4, S - STEP], BF16, name="plain1")
-        woven = sb.tile([P, S - STEP, 4], BF16, name="woven", tag="port", align_bytes=64)
+        woven_first = shared.tile([P, STEP, 4], BF16, name="woven_first", offset=0, align_bytes=64)
+        woven_rest = shared.tile([P, S - 2 * STEP, 4], BF16, name="woven_rest", offset=STEP * 4 * 2, align_bytes=64)
+        woven = {1: woven_first[:], 2: woven_rest[:, :STEP, :], 3: woven_rest[:, STEP:, :]}
         for j in range(3):
             nc.vector.tensor_copy(stepped[:, :, j], picked(rows[1, j], 0, STEP))
             nc.scalar.activation(plain1[:, j, :], picked(rows[1, j], STEP, S), ACT.Copy)
             if j == 1:
-                nc.gpsimd.tensor_scalar(woven[:, :, 0:2], side_by_side(plain1[:, 0:2, :]), 1.0, 0.0, ALU.mult, ALU.add)
+                nc.gpsimd.tensor_scalar(woven_first[:, :, 0:2], side_by_side(plain1[:, 0:2, :STEP]), 1.0, 0.0, ALU.mult, ALU.add)
+                nc.gpsimd.tensor_scalar(woven_rest[:, :, 0:2], side_by_side(plain1[:, 0:2, STEP:]), 1.0, 0.0, ALU.mult, ALU.add)
         nc.vector.tensor_copy(stepped[:, :, 3], picked(rows[1, 3], 0, STEP))
         nc.vector.tensor_copy(plain1[:, 3, S - STEP - SPARE :], picked(rows[1, 3], S - SPARE, S))
         for a, b in ((STEP, 2 * STEP), (2 * STEP, S - SPARE)):
             nc.scalar.activation(plain1[:, 3, a - STEP : b - STEP], picked(rows[1, 3], a, b), ACT.Copy)
         for a in range(0, S - STEP, STEP):
-            nc.scalar.copy(woven[:, a : a + STEP, 2:4], side_by_side(plain1[:, 2:4, a : a + STEP]))
+            nc.scalar.copy(woven[a // STEP + 1][:, :, 2:4], side_by_side(plain1[:, 2:4, a : a + STEP]))
 
-        def quantise_nodes(a):
-            i = max(n for n, (first, end) in enumerate(PIECES) if first <= a)
-            first, end = PIECES[i]
-            if a == first:
-                codes1[i] = sb.tile([P, end - first], U32, name="codes1_%d" % i, tag="w_bf0" if i == 1 else "codes1_%d" % i, align_bytes=64)
-            source = woven[:, a - STEP : a, :] if a else stepped[:]
-            quantise(codes1[i][:, a - first : a - first + STEP], scales[1][:, a : a + STEP], source)
+        def round_weights(g, groups):
+            nc.vector.tensor_copy(groups.rearrange("p (c i) j -> p c j i", i=4), w_raw[g][:].rearrange("p j (c i) -> p c j i", i=4))
 
-        for g in range(PASSES):
-            cols = slice(g * N, (g + 1) * N)
-            w_bf = sb.tile([P, N, 4], BF16, name="w_bf%d" % g, tag="w_bf%d" % g, align_bytes=64)
-            nc.vector.tensor_copy(w_bf[:].rearrange("p (c i) j -> p c j i", i=4), w_raw[g][:].rearrange("p j (c i) -> p c j i", i=4))
-            quantise_nodes(g * STEP)
-            quantise(w_codes[:, cols], w_scales[:, cols], w_bf[:])
+        def quantise_nodes(i):
+            if i == 1:
+                codes1[i] = sb.tile([P, STEP], U32, name="codes1_1", tag="joint", align_bytes=64)[:]
+            else:
+                codes1[i] = shared.tile([P, STEP], U32, name="codes1_%d" % i, offset=(i - 2) * STEP * 4, align_bytes=64)[:]
+            scales1[i] = sb.tile([P, STEP], U8, name="scales1_%d" % i, align_bytes=64)[:]
+            quantise(codes1[i], scales1[i], woven[i])
+
+        round_weights(0, joint[:, STEP:, :])
+        quantise(joint_codes[:], joint_scales[:], joint[:])
+        codes1[0], scales1[0] = joint_codes[:, :STEP], joint_scales[:, :STEP]
+        w_codes[0], w_scales[0] = joint_codes[:, STEP:], joint_scales[:, STEP:]
+        w_bf = sb.tile([P, N, 4], BF16, name="w_bf", align_bytes=64)
+        w_codes[1] = sb.tile([P, N], U32, name="w_codes1", align_bytes=64)[:]
+        w_scales[1] = sb.tile([P, N], U8, name="w_scales1", align_bytes=64)[:]
+        round_weights(1, w_bf[:])
+        quantise_nodes(1)
+        quantise(w_codes[1], w_scales[1], w_bf[:])
         for i in range(len(PIECES)):
             product(0, i)
-        for a in range(PASSES * STEP, S, STEP):
-            quantise_nodes(a)
+        for i in range(2, len(PIECES)):
+            quantise_nodes(i)
         for i, (a, b) in enumerate(PIECES):
             product(1, i)
             if i == 2:

@@ -51,7 +51,7 @@ def tile_picked_grand_relu_e_kernel(tc, xT, w1, gate, offs, cen, pos1, pos2, pos
             nc.sync.dma_start(out=rows[1, j], in_=x_rows[1, :, j, :])
         w_raw = []
         for g in range(PASSES):
-            w_raw.append(sb.tile([P, 4, N], F32, name="w_raw%d" % g, align_bytes=64))
+            w_raw.append(sb.tile([P, 4, N], F32, name="w_raw%d" % g, tag="w_raw%d" % g, align_bytes=64))
             nc.sync.dma_start(out=w_raw[g][:], in_=w_rows[g])
         lists = []
         for i, src in enumerate((cen, pos1, pos2, pos3, pos4)):
@@ -121,19 +121,19 @@ def tile_picked_grand_relu_e_kernel(tc, xT, w1, gate, offs, cen, pos1, pos2, pos
         stepped = joint[:, :STEP, :]
         plain1 = sb.tile([P, 4, S - STEP], BF16, name="plain1")
         woven_first = shared.tile([P, STEP, 4], BF16, name="woven_first", offset=0, align_bytes=64)
-        woven_rest = shared.tile([P, S - 2 * STEP, 4], BF16, name="woven_rest", offset=STEP * 4 * 2, align_bytes=64)
-        woven = {1: woven_first[:], 2: woven_rest[:, :STEP, :], 3: woven_rest[:, STEP:, :]}
+        woven_rest = shared.tile([P, STEP, 4], BF16, name="woven_rest", offset=STEP * 4 * 2, align_bytes=64)
+        woven = {1: woven_first[:], 2: woven_rest[:]}
         for j in range(3):
             nc.vector.tensor_copy(stepped[:, :, j], picked(rows[1, j], 0, STEP))
             nc.scalar.activation(plain1[:, j, :], picked(rows[1, j], STEP, S), ACT.Copy)
             if j == 1:
                 nc.gpsimd.tensor_scalar(woven_first[:, :, 0:2], side_by_side(plain1[:, 0:2, :STEP]), 1.0, 0.0, ALU.mult, ALU.add)
-                nc.gpsimd.tensor_scalar(woven_rest[:, :, 0:2], side_by_side(plain1[:, 0:2, STEP:]), 1.0, 0.0, ALU.mult, ALU.add)
+                nc.gpsimd.tensor_scalar(woven_rest[:, :, 0:2], side_by_side(plain1[:, 0:2, STEP : 2 * STEP]), 1.0, 0.0, ALU.mult, ALU.add)
         nc.vector.tensor_copy(stepped[:, :, 3], picked(rows[1, 3], 0, STEP))
         nc.vector.tensor_copy(plain1[:, 3, S - STEP - SPARE :], picked(rows[1, 3], S - SPARE, S))
         for a, b in ((STEP, 2 * STEP), (2 * STEP, S - SPARE)):
             nc.scalar.activation(plain1[:, 3, a - STEP : b - STEP], picked(rows[1, 3], a, b), ACT.Copy)
-        for a in range(0, S - STEP, STEP):
+        for a in range(0, 2 * STEP, STEP):
             nc.scalar.copy(woven[a // STEP + 1][:, :, 2:4], side_by_side(plain1[:, 2:4, a : a + STEP]))
 
         def round_weights(g, groups):
@@ -155,6 +155,8 @@ def tile_picked_grand_relu_e_kernel(tc, xT, w1, gate, offs, cen, pos1, pos2, pos
         w_codes[1] = sb.tile([P, N], U32, name="w_codes1", align_bytes=64)[:]
         w_scales[1] = sb.tile([P, N], U8, name="w_scales1", align_bytes=64)[:]
         round_weights(1, w_bf[:])
+        woven[3] = sb.tile([P, STEP, 4], BF16, name="woven_last", tag="w_raw0", align_bytes=64)[:]
+        nc.vector.tensor_copy(woven[3].rearrange("p (c i) j -> p c j i", i=4), plain1[:, :, 2 * STEP :].rearrange("p j (c i) -> p c j i", i=4))
         quantise_nodes(1)
         quantise(w_codes[1], w_scales[1], w_bf[:])
         for i in range(len(PIECES)):

@@ -20,6 +20,7 @@ GROUP = 16
 PASSES = K // (4 * P)
 SPLIT0 = 256
 SPARE = 64
+CAST_SPLIT = 80
 STEP = 128
 PIECES = ((0, 128), (128, 256), (256, 384), (384, 512))
 TURNED = ((1, 1), (0, 0), (0, 1), (2, 1), (2, 0), (1, 0))
@@ -136,8 +137,8 @@ def tile_picked_grand_relu_e_kernel(tc, xT, w1, gate, offs, cen, pos1, pos2, pos
         for a in range(0, 2 * STEP, STEP):
             nc.scalar.copy(woven[a // STEP + 1][:, :, 2:4], side_by_side(plain1[:, 2:4, a : a + STEP]))
 
-        def round_weights(g, groups):
-            nc.vector.tensor_copy(groups.rearrange("p (c i) j -> p c j i", i=4), w_raw[g][:].rearrange("p j (c i) -> p c j i", i=4))
+        def round_weights(copy, groups, raw):
+            copy(groups.rearrange("p (c i) j -> p c j i", i=4), raw.rearrange("p j (c i) -> p c j i", i=4))
 
         def quantise_nodes(i):
             if i == 1:
@@ -147,14 +148,15 @@ def tile_picked_grand_relu_e_kernel(tc, xT, w1, gate, offs, cen, pos1, pos2, pos
             scales1[i] = sb.tile([P, STEP], U8, name="scales1_%d" % i, align_bytes=64)[:]
             quantise(codes1[i], scales1[i], woven[i])
 
-        round_weights(0, joint[:, STEP:, :])
+        round_weights(nc.vector.tensor_copy, joint[:, STEP:, :], w_raw[0][:])
         quantise(joint_codes[:], joint_scales[:], joint[:])
         codes1[0], scales1[0] = joint_codes[:, :STEP], joint_scales[:, :STEP]
         w_codes[0], w_scales[0] = joint_codes[:, STEP:], joint_scales[:, STEP:]
         w_bf = sb.tile([P, N, 4], BF16, name="w_bf", align_bytes=64)
         w_codes[1] = sb.tile([P, N], U32, name="w_codes1", align_bytes=64)[:]
         w_scales[1] = sb.tile([P, N], U8, name="w_scales1", align_bytes=64)[:]
-        round_weights(1, w_bf[:])
+        round_weights(nc.vector.tensor_copy, w_bf[:, :CAST_SPLIT, :], w_raw[1][:, :, :CAST_SPLIT])
+        round_weights(nc.scalar.copy, w_bf[:, CAST_SPLIT:, :], w_raw[1][:, :, CAST_SPLIT:])
         woven[3] = sb.tile([P, STEP, 4], BF16, name="woven_last", tag="w_raw0", align_bytes=64)[:]
         nc.vector.tensor_copy(woven[3].rearrange("p (c i) j -> p c j i", i=4), plain1[:, :, 2 * STEP :].rearrange("p j (c i) -> p c j i", i=4))
         quantise_nodes(1)

@@ -19,7 +19,7 @@ P = 128
 GROUP = 16
 PASSES = K // (4 * P)
 SPLIT0 = 256
-SPARE = 64
+SPARE = 128
 CAST_SPLIT = 80
 STEP = 128
 PIECES = ((0, 128), (128, 256), (256, 384), (384, 512))
@@ -31,7 +31,6 @@ def tile_picked_grand_relu_e_kernel(tc, xT, w1, gate, offs, cen, pos1, pos2, pos
     with ExitStack() as ctx:
         sb = ctx.enter_context(tc.tile_pool(name="sb", bufs=1))
         ps = ctx.enter_context(tc.psum_pool(name="ps", bufs=1))
-        shared = ctx.enter_context(tc.tile_pool(name="shared", bufs=1))
 
         x_rows = xT.rearrange("(g p j) t -> g p j t", p=P, j=4)
         w_rows = w1.rearrange("(g p j) m -> g p j m", p=P, j=4)
@@ -106,7 +105,7 @@ def tile_picked_grand_relu_e_kernel(tc, xT, w1, gate, offs, cen, pos1, pos2, pos
                 stop=(g == PASSES - 1),
             )
 
-        groups0 = shared.tile([P, S, 4], BF16, name="groups0", offset=0, align_bytes=64)
+        groups0 = sb.tile([P, S, 4], BF16, name="groups0", tag="port", align_bytes=64)
         plain0 = sb.tile([P, 4, S - SPLIT0], F32, name="plain0")
         for j in range(4):
             nc.scalar.activation(plain0[:, j, :], picked(rows[0, j], SPLIT0, S), ACT.Copy)
@@ -116,20 +115,18 @@ def tile_picked_grand_relu_e_kernel(tc, xT, w1, gate, offs, cen, pos1, pos2, pos
                 nc.gpsimd.tensor_scalar(groups0[:, SPLIT0:, pair], side_by_side(plain0[:, pair, :]), 1.0, 0.0, ALU.mult, ALU.add)
         quantise(codes0[:], scales0[:], groups0[:])
 
-        joint = sb.tile([P, STEP + N, 4], BF16, name="joint", tag="joint", align_bytes=64)
+        joint = sb.tile([P, STEP + N, 4], BF16, name="joint", align_bytes=64)
         joint_codes = sb.tile([P, STEP + N], U32, name="joint_codes", align_bytes=64)
         joint_scales = sb.tile([P, STEP + N], U8, name="joint_scales", align_bytes=64)
         stepped = joint[:, :STEP, :]
         plain1 = sb.tile([P, 4, S - STEP], BF16, name="plain1")
-        woven_first = shared.tile([P, STEP, 4], BF16, name="woven_first", offset=0, align_bytes=64)
-        woven_rest = shared.tile([P, STEP, 4], BF16, name="woven_rest", offset=STEP * 4 * 2, align_bytes=64)
-        woven = {1: woven_first[:], 2: woven_rest[:]}
+        middle = sb.tile([P, 2 * STEP, 4], BF16, name="middle", tag="port", align_bytes=64)
+        woven = {1: middle[:, :STEP, :], 2: middle[:, STEP:, :]}
         for j in range(3):
             nc.vector.tensor_copy(stepped[:, :, j], picked(rows[1, j], 0, STEP))
             nc.scalar.activation(plain1[:, j, :], picked(rows[1, j], STEP, S), ACT.Copy)
             if j == 1:
-                nc.gpsimd.tensor_scalar(woven_first[:, :, 0:2], side_by_side(plain1[:, 0:2, :STEP]), 1.0, 0.0, ALU.mult, ALU.add)
-                nc.gpsimd.tensor_scalar(woven_rest[:, :, 0:2], side_by_side(plain1[:, 0:2, STEP : 2 * STEP]), 1.0, 0.0, ALU.mult, ALU.add)
+                nc.gpsimd.tensor_scalar(middle[:, :, 0:2], side_by_side(plain1[:, 0:2, : 2 * STEP]), 1.0, 0.0, ALU.mult, ALU.add)
         nc.vector.tensor_copy(stepped[:, :, 3], picked(rows[1, 3], 0, STEP))
         nc.vector.tensor_copy(plain1[:, 3, S - STEP - SPARE :], picked(rows[1, 3], S - SPARE, S))
         for a, b in ((STEP, 2 * STEP), (2 * STEP, S - SPARE)):
@@ -141,10 +138,7 @@ def tile_picked_grand_relu_e_kernel(tc, xT, w1, gate, offs, cen, pos1, pos2, pos
             copy(groups.rearrange("p (c i) j -> p c j i", i=4), raw.rearrange("p j (c i) -> p c j i", i=4))
 
         def quantise_nodes(i):
-            if i == 1:
-                codes1[i] = sb.tile([P, STEP], U32, name="codes1_1", tag="joint", align_bytes=64)[:]
-            else:
-                codes1[i] = shared.tile([P, STEP], U32, name="codes1_%d" % i, offset=(i - 2) * STEP * 4, align_bytes=64)[:]
+            codes1[i] = codes_rest[:, (i - 1) * STEP : i * STEP]
             scales1[i] = sb.tile([P, STEP], U8, name="scales1_%d" % i, align_bytes=64)[:]
             quantise(codes1[i], scales1[i], woven[i])
 
@@ -159,11 +153,11 @@ def tile_picked_grand_relu_e_kernel(tc, xT, w1, gate, offs, cen, pos1, pos2, pos
         round_weights(nc.scalar.copy, w_bf[:, CAST_SPLIT:, :], w_raw[1][:, :, CAST_SPLIT:])
         woven[3] = sb.tile([P, STEP, 4], BF16, name="woven_last", tag="w_raw0", align_bytes=64)[:]
         nc.vector.tensor_copy(woven[3].rearrange("p (c i) j -> p c j i", i=4), plain1[:, :, 2 * STEP :].rearrange("p j (c i) -> p c j i", i=4))
-        quantise_nodes(1)
         quantise(w_codes[1], w_scales[1], w_bf[:])
         for i in range(len(PIECES)):
             product(0, i)
-        for i in range(2, len(PIECES)):
+        codes_rest = sb.tile([P, S - STEP], U32, name="codes1_rest", tag="w_raw1", align_bytes=64)
+        for i in range(1, len(PIECES)):
             quantise_nodes(i)
         for i, (a, b) in enumerate(PIECES):
             product(1, i)

from contextlib import ExitStack

import concourse.mybir as mybir
from concourse.masks import make_identity

K, T, S, D, V, N = 1024, 1024, 512, 4, 256, 128
FLOPS = 2 * K * N * S

F32 = mybir.dt.float32
BF16 = mybir.dt.bfloat16
U32 = mybir.dt.uint32
U16 = mybir.dt.uint16
U8 = mybir.dt.uint8
FP8X4 = mybir.dt.float8_e4m3fn_x4
ACT = mybir.ActivationFunctionType
ALU = mybir.AluOpType

P = 128
GROUP = 16
PASSES = K // (4 * P)
SPLIT0 = 256
SPARE = 128
CAST_SPLIT = 80
STEP = 128
PIECES = ((0, 128), (128, 256), (256, 384), (384, 512))
TURNED = ((1, 1), (0, 0), (0, 1), (2, 1), (2, 0), (1, 0))


def tile_picked_grand_relu_e_kernel(tc, xT, w1, gate, offs, cen, pos1, pos2, pos3, pos4, out):
    nc = tc.nc
    with ExitStack() as ctx:
        sb = ctx.enter_context(tc.tile_pool(name="sb", bufs=1))
        ps = ctx.enter_context(tc.psum_pool(name="ps", bufs=1))

        x_rows = xT.rearrange("(g p j) t -> g p j t", p=P, j=4)
        w_rows = w1.rearrange("(g p j) m -> g p j m", p=P, j=4)

        offs_sb = sb.tile([P, S // GROUP], U16, name="offs_sb")
        gate_rows = sb.tile([P, V], F32, name="gate_rows")
        nc.gpsimd.memset(gate_rows[:], 0.0)
        rows = {}
        for j in (0, 2):
            two_rows = sb.tile([P, 2, T], F32, name="rows0_%d" % j)
            nc.sync.dma_start(out=two_rows[:], in_=x_rows[0, :, j : j + 2, :])
            rows[0, j], rows[0, j + 1] = two_rows[:, 0, :], two_rows[:, 1, :]
            if j == 0:
                nc.sync.dma_start(offs_sb[:], offs)
                nc.sync.dma_start(out=gate_rows[0:D, :], in_=gate[:, 0, :])
        for j in range(4):
            rows[1, j] = sb.tile([P, T], F32, name="row1_%d" % j)[:]
            nc.sync.dma_start(out=rows[1, j], in_=x_rows[1, :, j, :])
        w_raw = []
        for g in range(PASSES):
            w_raw.append(sb.tile([P, 4, N], F32, name="w_raw%d" % g, tag="w_raw%d" % g, align_bytes=64))
            nc.sync.dma_start(out=w_raw[g][:], in_=w_rows[g])
        lists = []
        for i, src in enumerate((cen, pos1, pos2, pos3, pos4)):
            lists.append(sb.tile([P, V // GROUP], U16, name="list%d" % i))
            nc.sync.dma_start(lists[i][:], src)
        gate_full = {}
        for i in (3, 4):
            gate_full[i] = sb.tile([P, V], F32, name="gate_full%d" % i)
            nc.sync.dma_start(out=gate_full[i][:], in_=gate[i - 1])

        eye = sb.tile([P, P], F32, name="eye")
        nc.vector.memset(eye[:, : P // 2], 0.0)
        nc.scalar.activation(eye[:, P // 2 :], eye[:, : P // 2], ACT.Copy)
        make_identity(nc, eye[:], nomemset=True)

        def quantise(packed, plane, groups):
            nc.vector.quantize_mx(out=packed.bitcast(FP8X4), scales=plane, in_=groups.rearrange("p n j -> p (n j)"))

        coef = sb.tile([P, 2, D], F32, name="coef")
        total = sb.tile([P, 2], F32, name="total")
        stay = sb.tile([P, 2], F32, name="stay")
        gate_bank = ps.tile([P, 2, P], F32, name="gate_bank", tag="bank0")
        for h in range(2):
            nc.tensor.transpose(gate_bank[:, h, :], gate_rows[:, h * P : (h + 1) * P], eye[:])
        for h in range(2):
            nc.scalar.activation(coef[:, h, :], gate_bank[:, h, 0:D], ACT.Copy, accum_out=total[:, h : h + 1])
        nc.scalar.activation(stay[:], total[:], ACT.Copy, scale=-1.0, bias=1.0)

        y = sb.tile([P, S], F32, name="y")
        acc = [ps.tile([P, b - a], F32, name="acc%d" % i, tag="acc%d" % i) for i, (a, b) in enumerate(PIECES)]
        codes0 = sb.tile([P, S], U32, name="codes0", align_bytes=64)
        codes1 = {}
        scales0 = sb.tile([P, S], U8, name="scales0", align_bytes=64)
        w_codes, w_scales, scales1 = {}, {}, {}

        def picked(row, a, b):
            return row.indirect(offs_sb[:, a // GROUP : b // GROUP])

        def side_by_side(plain):
            return plain.rearrange("p j n -> p n j")

        def product(g, i):
            a, b = PIECES[i]
            nc.tensor.matmul_mx(
                out=acc[i][:],
                lhsT=w_codes[g].bitcast(FP8X4),
                lhsT_scale=w_scales[g],
                rhs=(codes1[i] if g else codes0[:, a:b]).bitcast(FP8X4),
                rhs_scale=scales1[i] if g else scales0[:, a:b],
                start=(g == 0),
                stop=(g == PASSES - 1),
            )

        groups0 = sb.tile([P, S, 4], BF16, name="groups0", tag="port", align_bytes=64)
        plain0 = sb.tile([P, 4, S - SPLIT0], F32, name="plain0")
        for j in range(4):
            nc.scalar.activation(plain0[:, j, :], picked(rows[0, j], SPLIT0, S), ACT.Copy)
            nc.vector.tensor_copy(groups0[:, :SPLIT0, j], picked(rows[0, j], 0, SPLIT0))
            if j % 2:
                pair = slice(j - 1, j + 1)
                nc.gpsimd.tensor_scalar(groups0[:, SPLIT0:, pair], side_by_side(plain0[:, pair, :]), 1.0, 0.0, ALU.mult, ALU.add)
        quantise(codes0[:], scales0[:], groups0[:])

        joint = sb.tile([P, STEP + N, 4], BF16, name="joint", align_bytes=64)
        joint_codes = sb.tile([P, STEP + N], U32, name="joint_codes", align_bytes=64)
        joint_scales = sb.tile([P, STEP + N], U8, name="joint_scales", align_bytes=64)
        stepped = joint[:, :STEP, :]
        plain1 = sb.tile([P, 4, S - STEP], BF16, name="plain1")
        middle = sb.tile([P, 2 * STEP, 4], BF16, name="middle", tag="port", align_bytes=64)
        woven = {1: middle[:, :STEP, :], 2: middle[:, STEP:, :]}
        for j in range(3):
            nc.vector.tensor_copy(stepped[:, :, j], picked(rows[1, j], 0, STEP))
            nc.scalar.activation(plain1[:, j, :], picked(rows[1, j], STEP, S), ACT.Copy)
            if j == 1:
                nc.gpsimd.tensor_scalar(middle[:, :, 0:2], side_by_side(plain1[:, 0:2, : 2 * STEP]), 1.0, 0.0, ALU.mult, ALU.add)
        nc.vector.tensor_copy(stepped[:, :, 3], picked(rows[1, 3], 0, STEP))
        nc.vector.tensor_copy(plain1[:, 3, S - STEP - SPARE :], picked(rows[1, 3], S - SPARE, S))
        for a, b in ((STEP, 2 * STEP), (2 * STEP, S - SPARE)):
            nc.scalar.activation(plain1[:, 3, a - STEP : b - STEP], picked(rows[1, 3], a, b), ACT.Copy)
        for a in range(0, 2 * STEP, STEP):
            nc.scalar.copy(woven[a // STEP + 1][:, :, 2:4], side_by_side(plain1[:, 2:4, a : a + STEP]))

        def round_weights(copy, groups, raw):
            copy(groups.rearrange("p (c i) j -> p c j i", i=4), raw.rearrange("p j (c i) -> p c j i", i=4))

        def quantise_nodes(i):
            codes1[i] = codes_rest[:, (i - 1) * STEP : i * STEP]
            scales1[i] = sb.tile([P, STEP], U8, name="scales1_%d" % i, align_bytes=64)[:]
            quantise(codes1[i], scales1[i], woven[i])

        round_weights(nc.vector.tensor_copy, joint[:, STEP:, :], w_raw[0][:])
        quantise(joint_codes[:], joint_scales[:], joint[:])
        codes1[0], scales1[0] = joint_codes[:, :STEP], joint_scales[:, :STEP]
        w_codes[0], w_scales[0] = joint_codes[:, STEP:], joint_scales[:, STEP:]
        w_bf = sb.tile([P, N, 4], BF16, name="w_bf", align_bytes=64)
        w_codes[1] = sb.tile([P, N], U32, name="w_codes1", align_bytes=64)[:]
        w_scales[1] = sb.tile([P, N], U8, name="w_scales1", align_bytes=64)[:]
        round_weights(nc.vector.tensor_copy, w_bf[:, :CAST_SPLIT, :], w_raw[1][:, :, :CAST_SPLIT])
        round_weights(nc.scalar.copy, w_bf[:, CAST_SPLIT:, :], w_raw[1][:, :, CAST_SPLIT:])
        woven[3] = sb.tile([P, STEP, 4], BF16, name="woven_last", tag="w_raw0", align_bytes=64)[:]
        nc.vector.tensor_copy(woven[3].rearrange("p (c i) j -> p c j i", i=4), plain1[:, :, 2 * STEP :].rearrange("p j (c i) -> p c j i", i=4))
        quantise(w_codes[1], w_scales[1], w_bf[:])
        for i in range(len(PIECES)):
            product(0, i)
        codes_rest = sb.tile([P, S - STEP], U32, name="codes1_rest", tag="w_raw1", align_bytes=64)
        for i in range(1, len(PIECES)):
            quantise_nodes(i)
        for i, (a, b) in enumerate(PIECES):
            product(1, i)
            if i == 2:
                nc.vector.tensor_scalar_max(y[:, a:b], acc[i][:], 0.0)
            else:
                nc.scalar.activation(y[:, a:b], acc[i][:], ACT.Relu)

        sums = [ps.tile([P, P], F32, name="sums%d" % h) for h in range(2)]

        def looked_up(i, a, b):
            return y[:].indirect(lists[i][:, a // GROUP : b // GROUP])

        fetched = [sb.tile([P, V], F32, name="fetched%d" % i) for i in range(3)]
        nc.vector.tensor_copy(fetched[1][:, P:], looked_up(1, P, V))
        nc.vector.tensor_copy(fetched[2][:], looked_up(2, 0, V))
        for i, h in ((0, 0), (0, 1), (1, 0)):
            nc.scalar.activation(fetched[i][:, h * P : (h + 1) * P], looked_up(i, h * P, (h + 1) * P), ACT.Copy)
        turned = {}
        for n, (i, h) in enumerate(TURNED):
            turned[i, h] = ps.tile([P, P], F32, name="bank%d_%d" % (i, h), tag="bank%d" % n if n < 2 else "acc%d" % (n - 2))[:]
            nc.tensor.transpose(turned[i, h], fetched[i][:, h * P : (h + 1) * P], eye[:])
        for n, (i, h) in enumerate(TURNED):
            scaled = sb.tile([P, P], F32, name="scaled%d_%d" % (i, h))
            factor = stay[:, h : h + 1] if i == 0 else coef[:, h, i - 1 : i]
            nc.scalar.activation(scaled[:], turned[i, h], ACT.Copy, scale=factor)
            opens = all(other != h for term, other in TURNED[:n])
            closes = all(other != h for term, other in TURNED[n + 1 :])
            nc.tensor.matmul(sums[h][:], scaled[:], eye[:], start=opens, stop=closes, is_transpose=True)

        term3 = sb.tile([P, V], F32, name="term3")
        nc.vector.tensor_tensor(term3[:], looked_up(3, 0, V), gate_full[3][:], ALU.mult)
        term4 = [sb.tile([P, P], F32, name="term4_%d" % h) for h in range(2)]
        fused = [sb.tile([P, P], F32, name="fused%d" % h) for h in range(2)]
        for h in (1, 0):
            nc.vector.tensor_tensor(term4[h][:], looked_up(4, h * P, (h + 1) * P), gate_full[4][:, h * P : (h + 1) * P], ALU.mult)
        for h in (1, 0):
            nc.vector.tensor_tensor(fused[h][:], term3[:, h * P : (h + 1) * P], term4[h][:], ALU.add)
        for h in (1, 0):
            res = sb.tile([P, P], F32, name="res%d" % h)
            nc.vector.tensor_tensor(res[:], sums[h][:], fused[h][:], ALU.add)
            nc.sync.dma_start(out=out[:, h * P : (h + 1) * P], in_=res[:])
